import numpy as np, ml_dtypes
CORES = [6,15,38,47]
N = 4
BF = ml_dtypes.bfloat16
def gentries(a):
    return np.ascontiguousarray(a.reshape(8, 16, -1).transpose(0, 2, 1)).reshape(8, -1)
def gtable(e):
    e = np.asarray(e); return np.ascontiguousarray(e.reshape(8, -1, 16).transpose(0, 2, 1)).reshape(128, -1).astype(np.int32)
W, O, S, D, T, RO = 3072, 160, 48, 2, 2, 4
DS = D * S; L = O + DS
H = T * (RO - 1) // 2
def parts(rng, h, q, full=False):
    th = rng.random((N, 8, W)) < rng.choice(np.array([0.2, 0.3, 0.45]), (N, 8, 1))
    th[..., :DS] = full | (rng.random((N, 8, DS)) < 0.9); th[..., W - DS:] = full | (rng.random((N, 8, DS)) < 0.85)
    rt = DS + np.argsort(rng.random((N, 8, W - DS)), axis=-1)[..., :O]
    np.put_along_axis(th, rt, True, 2)
    order = DS + np.argsort(np.where(th, 2.0, 0.0)[..., DS:] + rng.random((N, 8, W - DS)), axis=-1)
    pos = np.zeros((N, 8, W), np.int64); np.put_along_axis(pos, order, np.arange(W - DS)[None, None, :], 2)
    nv = np.maximum(W - DS - np.sum(th[..., DS:], axis=-1), 1)[..., None, None]
    p = pos[..., None] - nv; u = rng.random((N, 8, W, 16))
    deep = (rng.random((N, 8, W, 16)) < rng.choice(q, (N, 8, W, 1))) & (p > 0)
    ix = np.where(deep, nv + (u * u * u * np.maximum(p, 0)).astype(np.int64), (u * nv).astype(np.int64))
    a = np.take_along_axis(order, ix.reshape(N, 8, 16 * W), 2).reshape(N, 8, W, 16)
    a = np.where(rng.random(a.shape) < h, rng.integers(0, DS, a.shape), a)
    return th, rt, a, order, nv
def fresh(rng, th, a, r, g):
    m = DS + rng.permutation(W - 2 * DS)
    th[r, g] = True; th[r, g, m[:24]] = False
    a[r, g] = m[rng.integers(0, 24, (W, 16))]
    return a[r, g], m[24:]
def chain(x, first, cells):
    c = np.concatenate([first[None, :], cells]); x[c[:-1], 0] = c[1:]
def values(rng):
    return np.clip(rng.integers(0, 16, (N, 8, 16, W)) + rng.integers(-4, 5, (N, 8, 1, W)), 0, 15)
def pack(th, rt, a, v):
    return {"ag": np.ascontiguousarray(a.transpose(0, 1, 3, 2)).reshape(N, 128, W).astype(np.int32), "vals": np.where(th[:, :, None, :], -1, v).reshape(N, 128, W).astype(np.float32).astype(BF),
            "rts": np.stack([gtable(x) for x in rt])}
def setup_inputs(rng):
    th, rt, a, order, nv = parts(rng, rng.choice(np.array([0.01, 0.02, 0.04]), (N, 8, 1, 1)), np.array([0.0, 0.08, 0.25]))
    return pack(th, rt, a, values(rng))
def setup_inputs_room(rng):
    th, rt, a, order, nv = parts(rng, 0.0, np.array([0.0, 0.0, 0.1]), True)
    for r in range(N):
        for g in range(4):
            lanes = rng.permutation(O); at = 0
            for d in range(D):
                n = int(rng.choice(np.array([0, 1, S - 1, S])))
                if r == 0 and d == 0: n = (S, 1, 0, S - 1)[g]
                a[r, g, rt[r, g, lanes[at:at + n]], 0] = d * S + rng.permutation(S)[:n]; at += n
    q = int(rng.integers(0, N)); j = np.arange(DS); early = np.isin(j % 4, np.array([1, 2]))
    for r in range(N):
        x, m = fresh(rng, th, a, r, 4); rt[r, 4] = m[:O]; m = m[O:]; d = (q - r) % N
        if d == 0:
            chain(x, rt[r, 4], m[:O * (T + H)].reshape(T + H, O)); m = m[O * (T + H):]
            chain(x, W - DS + j, m[:DS * H].reshape(H, DS))
        elif d <= D: x[rt[r, 4, :S], 0] = (d - 1) * S + rng.permutation(S)
        x, m = fresh(rng, th, a, r, 5); rt[r, 5] = m[:O]; m = m[O:]
        c = m[:T * DS].reshape(T, DS); chain(x, rt[r, 5, :DS], c); x[c[-1], 0] = rng.permutation(DS)
        s = rt[r, 5, DS:]; y = m[T * DS:T * DS + O - DS]; k = np.arange(O - DS) % 3
        x[s[k < 2], 0] = y[k < 2]; x[y[k == 0], 0] = s[k == 0]
        x[y[k == 1], 1] = s[k == 1]; x[y[k == 1], 8] = s[k == 1]; x[s[k == 2], 1] = s[k == 2]; x[s[k == 2], 8] = s[k == 2]
        x, m = fresh(rng, th, a, r, 6); rt[r, 6] = m[:O]; m = m[O:]; th[r, 6, W - DS:] = False
        s = rt[r, 6, :DS]; c = m[:H * DS].reshape(H, DS); x[s, 0] = rng.permutation(DS); x[s, 1] = c[0]; x[s, 8] = c[0]; chain(x, c[0], c[1:])
        x, m = fresh(rng, th, a, r, 7); rt[r, 7] = m[:O]; m = m[O:]; n = DS // 2
        s = rt[r, 7, :DS]; e = W - DS + j; c = m[:T * n].reshape(T, n); m = m[T * n:]; f = m[:T * n].reshape(T, n); z = m[T * n:T * n + n]
        x[s[early], 0] = j[early]; chain(x, s[~early], c); x[c[-1], 0] = j[~early]
        chain(x, e[early], f); x[f[-1], 0] = z[j[early] // 2]; x[e[~early], 0] = z[j[~early] // 2]; x[z, 0] = z
    return pack(th, rt, a, values(rng))
def setup_inputs_crowd(rng):
    th, rt, a, order, nv = parts(rng, 0.01, np.array([0.0, 0.1]), True); n_ = np.arange(N)[:, None]
    for g in range(8):
        k = nv[:, g, :, 0] + rng.integers(0, 4, (N, O)); hot = np.take_along_axis(order[:, g], k, 1)
        if g == 1: hot = np.full((N, O), W - 1)
        if g == 2: hot[:, 1:] = rt[:, g, :-1]
        if g == 3: hot = np.where(rng.random((N, O)) < 0.5, 0, DS - 1)
        if g == 5:
            hot[:, :DS] = np.arange(DS)
            for r in range(N):
                x = a[r, g]; v0 = order[r, g, 0]
                u = order[r, g, nv[r, g, 0, 0]:]; u = u[(u < W - DS) & ~np.isin(u, rt[r, g])]; f = u[-T - 1:]
                x[np.isin(x, f)] = v0
                x[u[:4]] = np.where(x[u[:4]] >= W - DS, v0, x[u[:4]])
                x[W - DS:, 0] = f[T]; x[f[:-1], 0] = f[1:]
                hot[r, DS:] = u[rng.integers(0, 4, O - DS)]; hot[r, O - 1] = f[0]
        a[n_, g, rt[:, g], 0] = np.where((rng.random((N, O)) < 0.8) | (g == 5), hot, a[n_, g, rt[:, g], 0])
    a[:, 1, W - 1] = order[:, 1, :16]
    return pack(th, rt, a, values(rng))
def setup_inputs_halves(rng):
    th, rt, a, order, nv = parts(rng, 0.02, np.array([0.0, 0.1, 0.2]))
    o = np.argsort(rng.random((N, 8, 16, W), dtype=np.float32), axis=2); k = rng.choice(np.array([0, 7, 8, 8, 9, 9, 10, 16]), (N, 8, 1, W))
    v = np.where(o < k, rng.choice(np.array([8, 8, 15]), (N, 8, 1, W)), rng.choice(np.array([0, 7, 7]), (N, 8, 1, W)))
    a[:, 4, :, 9:] = a[:, 4, :, 8:9]; a[:, 5, :, 1:8] = a[:, 5, :, 1:2]; a[:, 6] = a[:, 6, :, 0:1]
    a[:, 7] = np.where(rng.random((N, W, 16)) < 0.1, rng.choice(np.array([0, DS - 1, DS, W - DS, W - 1]), (N, W, 16)), a[:, 7])
    return pack(th, rt, a, v)
def setup_inputs_rings(rng):
    th, rt, a, order, nv = parts(rng, 0.01, np.array([0.0, 0.1]), True); n_ = np.arange(N)[:, None]
    for g in (0, 2, 4, 6): a[n_, g, order[:, g, 1:], 0] = order[:, g, :-1]
    for g in (1, 3, 5):
        e = np.arange(0, DS, 1 if g < 4 else 2)[None, :]
        a[n_, g, W - DS + e, 0] = (e + g * S) % DS
        a[n_, g, rt[:, g, :DS], 0] = np.arange(DS)[None, :]
        x = rt[:, g, DS:DS + 8]; a[n_, g, x, 0] = x
        x = rt[:, g, DS + 8:DS + 16]; a[n_, g, x, 0] = x[:, ::-1]
    k = (DS - 1 - np.arange(DS)) % 3; n = min(DS, O - DS)
    for r in range(N):
        x, m = fresh(rng, th, a, r, 7); e = W - DS + rng.permutation(DS)
        rt[r, 7] = np.concatenate([e, m[:O - DS]]); x[m[:n], 0] = rng.permutation(DS)[:n]; m = m[O - DS:]
        x[e[k == 0], 0] = np.roll(e[k == 0], 1)
        up = e[k == 1]; chain(x, up, m[:(T - 1) * len(up)].reshape(T - 1, len(up)))
    return pack(th, rt, a, values(rng))
def setup_inputs_spread(rng):
    th, rt, a, order, nv = parts(rng, rng.choice(np.array([0.002, 0.02, 0.1]), (N, 8, 1, 1)), np.array([0.0, 0.05, 0.15, 0.5]))
    v = np.minimum((np.exp2(4 * rng.random((N, 8, 1, W))) * rng.random((N, 8, 16, W))).astype(np.int64), 15)
    return pack(th, rt, a, np.where(rng.random((N, 8, 1, W)) < 0.5, v, 15 - v))
def check_inputs(d):
    bad = []
    v = np.asarray(d["vals"]).astype(np.float32).reshape(N, 8, 16, W); r = np.stack([gentries(x) for x in d["rts"]])
    if np.min(d["ag"]) < 0 or np.max(d["ag"]) > W - 1: bad.append("range of ag")
    if not np.all((v == np.floor(v)) & (v >= -1) & (v <= 15)): bad.append("whole numbers of vals")
    if np.any(np.any(v < 0, axis=2) != np.all(v < 0, axis=2)): bad.append("thunks are -1 in all 16 rows")
    s = np.sort(r, axis=-1)
    if np.any(s[..., 1:] == s[..., :-1]): bad.append("starting cells differ")
    if np.min(r) < DS or np.max(r) > W - 1: bad.append("range of rts")
    elif not np.all(np.take_along_axis(v[:, :, 0], r.astype(np.int64), 2) == -1): bad.append("starting cells are thunks")
    return bad
def reference(ag, vals, rts):
    B = N * 8; i16 = np.arange(16)
    arg = np.stack([gentries(x) for x in ag]).reshape(B, W, 16).astype(np.int64)
    val = vals.astype(np.float32).astype(np.int16).reshape(B, 16, W)
    cur = np.full((B, L), -1, np.int64)
    cur[:, :O] = np.stack([gentries(x) for x in rts]).reshape(B, O)
    par = np.full((B, W), -1, np.int64)
    np.put_along_axis(val, cur[:, None, :O], -2, 2)
    rows = np.arange(B)[:, None]; lane = np.arange(L)[None, :]
    for rnd in range(RO):
        for step in range(T):
            act = cur >= 0; c = np.maximum(cur, 0)
            a = arg[rows, c]
            v = np.take_along_axis(val, a.reshape(B, 1, L * 16), 2).reshape(B, 16, L, 16)
            st = v[:, 0]; s = v[..., 0]; has = st[..., 0] >= 0
            many = np.sum(s >= 8, axis=1) >= 9
            need = np.where(~has[..., None], i16 == 0, np.where(many[..., None], (i16 >= 1) & (i16 < 8), i16 >= 8))
            lack = need & (st < 0); stop = np.any(lack, axis=-1); first = np.argmax(lack, axis=-1)[..., None]
            to = np.take_along_axis(a, first, 2)[..., 0]; kind = np.take_along_axis(st, first, 2)[..., 0]
            want = act & stop & (kind == -1); done = act & ~stop
            lead = np.full((B, W), L, np.int64); b, k = np.nonzero(want); np.minimum.at(lead, (b, to[b, k]), k)
            win = want & (np.take_along_axis(lead, to, 1) == lane); ent = win & (to >= DS)
            res = np.maximum(np.max(np.where(need[:, None], v, -9), axis=-1) - s, 0)
            b, k = np.nonzero(done); val[b, :, c[b, k]] = res[b, :, k]
            b, k = np.nonzero(win); val[b, :, to[b, k]] = -2
            cur = np.where(ent, to, np.where(done, np.take_along_axis(par, c, 1), cur))
            b, k = np.nonzero(ent); par[b, to[b, k]] = c[b, k]
        if rnd < RO - 1:
            old = np.array(val).reshape(N, 8, 16, W); new = np.array(old); c4 = cur.reshape(N, 8, L)
            for r in range(N):
                for d in range(1, D + 1):
                    q = (r + d) % N; lo = (d - 1) * S; e = W - DS + lo
                    asked = old[r, :, 0, lo:lo + S] == -2; ev = old[q, :, :, e:e + S]
                    home = asked & (ev[:, 0] >= 0); go = asked & (ev[:, 0] == -1)
                    new[r, :, :, lo:lo + S] = np.where(home[:, None, :], ev, old[r, :, :, lo:lo + S])
                    new[q, :, :, e:e + S] = np.where(go[:, None, :], -2, ev)
                    c4[q, :, O + lo:O + lo + S] = np.where(go, e + np.arange(S)[None, :], c4[q, :, O + lo:O + lo + S])
            val = new.reshape(B, 16, W); cur = c4.reshape(B, L)
    return {"yv": val.reshape(N, 128, W).astype(np.float32).astype(BF), "ya": np.stack([gtable(x) for x in cur.reshape(N, 8, L)]).astype(np.float32)}

@@ -1,0 +1,539 @@
+from concourse.bass import DstId, RemoteDMATransfer
+from concourse.mybir import AluOpType, ActivationFunctionType
+
+OP = AluOpType
+AF = ActivationFunctionType
+W, OWN, BLK, DS, LANES, NR = 3072, 160, 48, 96, 256, 4
+WT = W + LANES
+HOLE, THUNK = 31.0, 32.0
+HALF = 1536
+TOL = 2.0 ** -10
+BIG = 2.0 ** 23
+KV = {160: 4, 256: 8}
+SPLIT = {160: (34, 30, 16), 256: (56, 48, 24)}
+
+F32, BF, F16, I32, U16 = "float32", "bfloat16", "float16", "int32", "uint16"
+
+
+def _sb(n, d):
+    return ("sbuf", [128, n], d)
+
+
+SCRATCH = {
+    "AG": _sb(WT, I32), "VR": _sb(W, BF), "U": _sb(WT, BF), "OUT": _sb(WT, BF),
+    "rti": _sb(16, I32), "rtf": _sb(16, F32),
+    "pi": _sb(8, I32), "pc": _sb(32, F32), "io_c": _sb(144, BF), "io_s": _sb(256, BF), "io_g": _sb(128, BF),
+    "io_h": _sb(128, BF), "io_t": _sb(896, BF), "io_k": _sb(96, F32),
+    "Wsl": _sb(144, F16), "Wd": _sb(144, F16), "Wf": _sb(144, F16), "Wy": _sb(128, F16), "W0": _sb(128, F16), "Wz": _sb(128, BF),
+    "Wlo": _sb(128, BF), "Whi": _sb(128, BF), "Wc": _sb(128, BF), "Ip": _sb(128, BF), "In": _sb(128, BF),
+    "Wr": _sb(128, F32), "ones": _sb(256, BF), "lad": _sb(896, BF), "nm": _sb(256, BF), "keep": _sb(256, BF),
+    "head": _sb(256, BF), "md": _sb(256, BF), "am": _sb(96, BF), "mE": _sb(576, BF), "zo": _sb(4, U16), "hol": _sb(160, BF),
+    "ecf": _sb(16, F32), "ec16": _sb(16, U16), "edf": _sb(16, F32), "slE": _sb(16, F32), "slf": _sb(16, F32), "dsl": _sb(16, F32),
+    "A": _sb(256, F16), "AE": _sb(96, F16), "sl16": _sb(16, U16), "ind": _sb(256, BF), "sv": _sb(256, BF),
+    "tm": _sb(128, F32), "t2": _sb(128, F32), "O16": _sb(128, U16), "V": _sb(2048, BF), "SO": _sb(2048, BF),
+    "m": _sb(256, BF), "y": _sb(256, F16), "tb": _sb(256, BF), "ab": _sb(256, BF), "dat": _sb(256, BF), "tn": _sb(256, BF),
+    "hold": _sb(256, F32), "bia": _sb(16, F32), "eq": _sb(256, BF),
+    "SD": _sb(256, BF), "E": _sb(576, BF), "Z": _sb(592, BF), "junk": _sb(4096, BF), "acc": _sb(16, F32),
+    "ST": _sb(112, F32), "DL": _sb(112, F32), "dn": _sb(16, F32), "s1": _sb(16, F32), "s2": _sb(16, F32),
+    "s3": _sb(16, F32), "s4": _sb(16, F32), "s5": _sb(16, F32), "s6": _sb(16, F32), "ri": _sb(16, I32),
+    "WN": _sb(32, F32), "ee": _sb(32, F32), "NX": _sb(32, F32),
+    "co": _sb(32, U16), "ent": _sb(16, F32), "pa": _sb(64, F32), "pb": _sb(64, F32),
+    "L0": _sb(192, BF), "L1": _sb(192, BF), "L2": _sb(192, BF), "stg": _sb(96, BF),
+    "xc": _sb(96, BF), "xd": _sb(96, BF), "xe": _sb(96, BF), "xf": _sb(96, BF), "xg": _sb(96, BF),
+    "yo": _sb(16, F32),
+    "Pq": ("psum", [128, 512], F32), "Pr": ("psum", [128, 512], F32), "Pc": ("psum", [128, 512], F32),
+    "Po": ("psum", [128, 512], F32), "Ps": ("psum", [128, 512], F32), "Pd": ("psum", [128, 512], F32),
+    "Pe": ("psum", [128, 512], F32), "Pf": ("psum", [128, 512], F32),
+}
+SEMAPHORES = (["qv", "qs", "qt", "qg"] + [n + str(x) for n in ("near", "far", "arr") for x in range(3)]
+              + ["d%d" % i for i in range(12)])
+
+
+def build(core, T, topo):
+    ops = []
+    rank = T.rank_of(core)
+
+    def add(q, fn, r, w, kind="c"):
+        ops.append((q, fn, list(r), list(w), kind))
+
+    def ts(out, in0, s1, o0, r, w, s2=None, o1=None):
+        if o1 is None:
+            add("v", lambda e: e.tensor_scalar(out, in0, s1, None, o0), r, w)
+        else:
+            add("v", lambda e: e.tensor_scalar(out, in0, s1, s2, o0, o1), r, w)
+
+    def tt(out, a, b, o, r, w):
+        add("v", lambda e: e.tensor_tensor(out, a, b, o), r, w)
+
+    def cp(out, a, r, w):
+        add("v", lambda e: e.tensor_copy(out, a), r, w)
+
+    def ms(out, c, w):
+        add("v", lambda e: e.memset(out, c), [], w)
+
+    def scan(out, d0, d1, o0, o1, r, w):
+        add("v", lambda e: e.tensor_tensor_scan(out, d0, d1, 0.0, o0, o1), r, w)
+
+    def act(out, a, f, r, w, bias=0.0, scale=1.0, acc=None):
+        add("s", lambda e: e.activation(out, a, f, bias=bias, scale=scale, accum_out=acc), r, w)
+
+    def mm(out, l, rh, st, sp, r, w):
+        add("t", lambda e: e.matmul(out, l, rh, st, sp), r, w)
+
+    def iota(out, pat, base, cm, w, flt=True):
+        if flt:
+            add("g", lambda e: e.iota(out, pat, base, cm, allow_small_or_imprecise_dtypes=True), [], w)
+        else:
+            add("g", lambda e: e.iota(out, pat, base, cm), [], w)
+
+    def dma(q, out, a, r, w, accum=False):
+        if accum:
+            add(q, lambda e: e.dma_start(out, a, accum_op=OP.add), r, w, "d")
+        else:
+            add(q, lambda e: e.dma_start(out, a), r, w, "d")
+
+    U, AG, pc = T.U, T.AG, T.pc
+    Uw = U[:, 0:WT]
+    UK = ["U0", "U1", "U2", "U3", "U4", "U5", "Ur", "Um"]
+    OK = ["O0", "O1", "O2", "O3", "Or"]
+    MID = ((DS, HALF), (HALF, W - DS))
+
+    def col(j):
+        return pc[:, j:j + 1]
+
+    dma("y", T.rti[:, 0:10], T.rts[:], [], ["rti"])
+    dma("y", T.VR[:, 0:HALF], T.vals[:, 0:HALF], [], ["VR0"])
+    dma("y", T.VR[:, HALF:W], T.vals[:, HALF:W], [], ["VR1"])
+    dma("y", AG[:, 0:W], T.ag[:], [], ["AG"])
+
+    def aff(j, src, rk, scale, bias):
+        act(col(j), src, AF.Identity, rk, ["c%d" % j], bias=bias, scale=scale)
+
+    iota(T.pi[:, 0:1], [[0, 1]], 0, 1, ["pi0"], False)
+    iota(T.io_c[:], [[1, 144]], 0, 0, ["io_c"])
+    iota(T.io_k[:], [[0, 6], [16, 16]], 0, 0, ["io_k"])
+    iota(T.io_h[:], [[1, 16], [0, 8]], 0, 0, ["io_h"])
+    iota(T.io_g[:], [[1, 8], [0, 16]], 0, 0, ["io_g"])
+    iota(T.io_s[:], [[0, 16], [1, 16]], 0, 0, ["io_s"])
+    iota(AG[:, W:WT], [[0, LANES]], W, 0, ["AGr"], False)
+    iota(T.io_t[:], [[0, 112], [1, 8]], 0, 0, ["io_t"])
+    ms(U[:, W:WT], HOLE, ["Ur"])
+    ms(T.hol[:], HOLE, ["hol"])
+    ms(T.ones[:], 1.0, ["ones"])
+    ts(T.pi[:, 1:2], T.pi[:, 0:1], 15, OP.bitwise_and, ["pi0"], ["pi1"])
+    ts(T.pi[:, 2:3], T.pi[:, 0:1], 4, OP.logical_shift_right, ["pi0"], ["pi2"])
+    ts(T.pi[:, 3:4], T.pi[:, 0:1], 7, OP.bitwise_and, ["pi0"], ["pi3"])
+    ms(T.acc[:], 0.0, ["acc"])
+    cp(pc[:, 0:4], T.pi[:, 0:4], ["pi0", "pi1", "pi2", "pi3"], ["c0"])
+    P, I, G, TT = col(0), col(1), col(2), col(3)
+    c0 = ["c0"]
+    ms(T.Z[:, 0:16], -TOL, ["Zc"])
+    ms(T.Z[:, 16:592], 0.0, ["Z"])
+    ts(col(6), I, 0.0, OP.is_equal, c0, ["c6"])
+    ts(col(9), I, 8.0, OP.is_ge, c0, ["c9"])
+    ts(col(13), I, 1.0, OP.is_equal, c0, ["c13"], 8192.0, OP.mult)
+    aff(7, P, c0, 1.0, 15.0)
+    aff(4, G, c0, 16.0, 15.0)
+    aff(11, G, c0, 2.0, 0.0)
+    aff(12, G, c0, 2.0, 1.0)
+    aff(5, I, ["c0", "c7"], -2.0, col(7))
+    aff(8, TT, ["c0", "c4"], -1.0, col(4))
+    aff(10, col(9), ["c9"], -2.0, 1.0)
+    aff(14, col(6), ["c6", "c13"], -131072.0, col(13))
+    aff(15, col(13), ["c13"], 192.0 / 8192.0, 0.0)
+    aff(18, col(6), ["c6"], -1.875, 2.0)
+    aff(19, col(6), ["c6"], 15.0, 16.0)
+    aff(20, TT, c0, 2.0, 18.0)
+    aff(25, I, c0, 8.0, 8.0)
+    aff(17, col(6), ["c6", "c15"], 491520.0, col(15))
+    aff(21, col(6), ["c6", "c20"], 13.125, col(20))
+    aff(26, col(25), ["c25", "c0"], I, 0.0)
+    aff(22, col(9), ["c9", "c21"], -100.0, col(21))
+    aff(16, col(21), ["c21"], 1.0, -100.0)
+    aff(24, I, c0, -1.0, 15.0)
+    aff(23, col(9), ["c9", "c16"], 100.0, col(16))
+    act(T.keep[:], T.io_s[:], AF.Tanh, ["io_s"], ["keep"], scale=20.0)
+    ms(T.SD[:], 0.0, ["SD"])
+    ms(T.hold[:, OWN:LANES], 1.0e5, ["hold"])
+    ms(T.mE[:], 2.0, ["mE"])
+    ts(T.Wr[:], T.io_c[:, 0:128], col(5), OP.is_equal, ["io_c", "c5"], ["Wr"])
+    ts(T.ST[:, 16:112], T.io_k[:], I, OP.add, ["io_k", "c0"], ["cur", "S"], float(W), OP.add)
+    ms(T.mE[:, 0:17:16], -1.0, ["mE"])
+    ts(T.Wsl[:], T.io_c[:], col(7), OP.is_equal, ["io_c", "c6", "c7"], ["Wsl"], col(6), OP.mult)
+    ts(T.Ip[:], T.io_c[:, 0:128], P, OP.is_equal, ["io_c", "c0"], ["Ip"])
+    ms(T.mE[:, 48:97:48], -1.0, ["mE"])
+    ts(T.In[:], T.io_c[:, 0:128], P, OP.is_equal, ["io_c", "c0"], ["In"], -1.0, OP.mult)
+    cp(T.rtf[:, 0:10], T.rti[:, 0:10], ["rti"], ["rtf"])
+    mm(T.Pe[:, 0:10], T.Wr[:], T.rtf[:, 0:10], True, True, ["Wr", "rtf"], ["Pe"])
+    ts(T.Wd[:], T.io_c[:], col(8), OP.is_equal, ["io_c", "c8", "c10"], ["Wd"], col(10), OP.mult)
+    ts(T.Wf[:], T.io_c[:], col(8), OP.is_equal, ["io_c", "c8", "c9"], ["Wf"], col(9), OP.mult)
+    ts(T.Wlo[:], T.io_h[:], col(11), OP.is_equal, ["io_h", "c11"], ["Wlo"])
+    ts(T.Whi[:], T.io_h[:], col(12), OP.is_equal, ["io_h", "c12"], ["Whi"])
+    ts(T.Wy[:], T.io_g[:], G, OP.is_equal, ["io_g", "c0"], ["Wy"])
+    ts(T.Wz[:], T.io_g[:], G, OP.is_equal, ["io_g", "c0", "c14"], ["Wz"], col(14), OP.mult)
+    cp(T.ST[:, 16:26], T.Pe[:, 0:10], ["Pe"], ["cur"])
+    ts(T.Wc[:], T.ones[:, 0:128], col(17), OP.mult, ["ones", "c17"], ["Wc"])
+    cp(T.co[:, 0:16], T.ST[:, 16:32], ["cur"], ["co"])
+    ts(T.nm[:], T.io_s[:], I, OP.not_equal, ["io_s", "c0"], ["nm"], BIG, OP.mult)
+    ts(T.md[:], T.io_s[:], I, OP.is_gt, ["io_s", "c0"], ["md"])
+    ts(T.W0[:], T.io_g[:], G, OP.is_equal, ["io_g", "c0", "c6"], ["W0r"], col(6), OP.mult)
+    mm(T.Ps[:, 0:OWN], T.Ip[:], T.nm[:, 0:OWN], True, False, ["Ip", "nm"], ["Ps"])
+
+    def ends(n, nl):
+        ts(col(27), I, KV[nl] + 0.5, OP.is_lt, ["c0", "c26"], ["c27"], col(26), OP.mult)
+        ts(T.zo[:, 2 * n:2 * n + 1], col(27), 15.0, OP.add, ["c27"], ["zo%d" % n])
+
+    ends(0, 160)
+    banks = ((T.Pq, "Pq"), (T.Pr, "Pr"), (T.Pc, "Pc"), (T.Po, "Po"), (T.Pd, "Pd"), (T.Pf, "Pf"))
+    for k, (pb, pk) in enumerate(banks):
+        act(pb[:], T.VR[:, 512 * k:512 * k + 512], AF.Relu, ["VR%d" % (k // 3)], [pk], scale=-THUNK)
+    for k, (pb, pk) in enumerate(banks):
+        tt(U[:, 512 * k:512 * k + 512], T.VR[:, 512 * k:512 * k + 512], pb[:], OP.max, ["VR%d" % (k // 3), pk], ["U%d" % k])
+    act(T.lad[:], T.io_t[:], AF.Identity, ["io_t", "c18", "c19"], ["lad"], bias=col(19), scale=col(18))
+    act(T.head[:], T.keep[:], AF.Identity, ["keep"], ["head"], bias=2.0 * BIG, scale=-2.0 * BIG)
+    cp(Uw.indirect(T.co[:, 0:10]), T.hol[:], ["co", "hol"] + UK, UK)
+    ms(T.lad[:, 0::8], 0.0, ["lad"])
+
+    def exchange_constants():
+        ts(T.ecf[:, 0:6], T.io_k[:, 0:6], I, OP.subtract, ["io_k", "c0"], ["ecf"], float(W - DS + 15), OP.add)
+        ts(T.am[:], T.io_s[:, 0:96], col(24), OP.is_equal, ["io_s", "c24"], ["am"])
+        cp(T.ec16[:, 0:6], T.ecf[:, 0:6], ["ecf"], ["ec16"])
+        tt(T.edf[:, 0:6], T.ecf[:, 0:6], T.ST[:, 106:112], OP.subtract, ["ecf", "S"], ["edf"])
+        ends(1, 256)
+        for k in range(5, KV[256] + 1):
+            ms(T.mE[:, 8 * k * (k - 1):8 * k * (k - 1) + 1], -1.0, ["mE"])
+
+    def gather_args(k0, k1, key):
+        ts(T.A[:, 16 * k0:16 * k1], AG[:, 0:WT].indirect(T.co[:, k0:k1]), float(HALF), OP.subtract,
+           ["AG", "AGr", "co"], key)
+
+    def list_arg0(src, nl, key):
+        for r in range(16):
+            mm(T.Ps[:, 0:nl // 16], T.Wsl[:, 15 - r:143 - r], src[:, r:nl:16], r == 0, r == 15, ["Wsl"] + key, ["Ps"])
+
+    def fold_args(l0, l1, key):
+        for n, wt, wk in ((0, T.Wd, "Wd"), (128, T.Wf, "Wf")):
+            for h in range(2):
+                mm(T.Po[:, n + l0 // 2:n + l1 // 2], wt[:, 8 - 8 * h:136 - 8 * h], T.A[:, l0 + h:l1:2], h == 0, h == 1,
+                   [wk] + key, ["Po"])
+
+    def deltas(depth):
+        n = 16 * (depth + 1)
+        tt(T.DL[:, 32:32 + n], T.ST[:, 16:16 + n], T.ST[:, 32:32 + n], OP.subtract, ["cur", "S"], ["DL"])
+
+    def stack_ops(depth):
+        o = [lambda: ts(T.ent[:], T.ee[:, 0:16], 0.0, OP.not_equal, ["ee"], ["ent"]),
+             lambda: cp(T.ST[:, 16:32], T.NX[:, 0:16], ["NX"], ["cur"])]
+        for d in range(1, depth + 1):
+            o.append(lambda d=d: tt(T.pb[:, 16 * d - 16:16 * d], T.dn[:], T.DL[:, 16 * d + 32:16 * d + 48], OP.mult,
+                                    ["dn", "DL"], ["pb%d" % d]))
+            o.append(lambda d=d: tt(T.pa[:, 16 * d - 16:16 * d], T.ent[:], T.DL[:, 16 * d + 16:16 * d + 32], OP.mult,
+                                    ["ent", "DL"], ["pa%d" % d]))
+        n = 16 * depth
+        o.append(lambda: tt(T.ST[:, 32:32 + n], T.ST[:, 32:32 + n], T.pb[:, 0:n], OP.subtract,
+                            ["S"] + ["pb%d" % d for d in range(1, depth + 1)], ["S"]))
+        o.append(lambda: tt(T.ST[:, 32:32 + n], T.ST[:, 32:32 + n], T.pa[:, 0:n], OP.add,
+                            ["S"] + ["pa%d" % d for d in range(1, depth + 1)], ["S"]))
+        return o
+
+    def unfold_ends():
+        for k, a, uk, tmp, tk in ((2, 0, "U0", T.xc, "xc"), (3, W - DS, "U5", T.xd, "xd")):
+            ts(tmp[:], U[:, a:a + DS], 16.0, OP.is_ge, [uk], [tk], -33.0, OP.mult)
+        for k, a, uk, tmp, tk in ((2, 0, "U0", T.xc, "xc"), (3, W - DS, "U5", T.xd, "xd")):
+            tt(T.OUT[:, a:a + DS], U[:, a:a + DS], tmp[:], OP.add, [uk, tk], ["O%d" % k])
+
+    def hole_flags():
+        ts(T.tn[:], T.SO[:, 7:2048:8], 16.0, OP.is_ge, ["R0", "R1", "R2"], ["tn"], -33.0, OP.mult)
+
+    def scatter_out():
+        tt(T.OUT[:, 0:WT].indirect(T.co[:, 16:32]), T.dat[:], T.tn[:], OP.add, ["co", "dat", "tn"] + OK, OK)
+
+    def step(t, nl, fill0, fill1, fill2):
+        M, KC, kv = nl // 2, nl // 16, KV[nl]
+        depth = min(t, 8 - t)
+        kh = (KC + 2) // 4 * 2
+        ts(T.ind[:, 0:16 * kh], Uw.indirect(T.sl16[:, 0:kh]), 8.0, OP.is_ge, UK + ["sl16"], ["ind0"], 0.5, OP.subtract)
+        act(T.ind[:, 16 * kh:nl], Uw.indirect(T.sl16[:, kh:KC]), AF.Sign, UK + ["sl16"], ["ind1"], bias=-7.5)
+        act(T.sv[:, 0:nl], Uw.indirect(T.sl16[:, 0:KC]), AF.Copy, UK + ["sl16"], ["sv"])
+        mm(T.Pc[:, 0:M], T.Wlo[:], T.ind[:, 0:nl:2], True, False, ["Wlo", "ind0", "ind1"], ["Pc"])
+        mm(T.Pc[:, 0:M], T.Whi[:], T.ind[:, 1:nl:2], False, True, ["Whi", "ind0", "ind1"], ["Pc"])
+        for f in fill0:
+            f()
+        for pq, pk in ((T.Pf, "Pf"), (T.Pq, "Pq"), (T.Pr, "Pr")):
+            mm(pq[:, 0:nl], T.Wc[:], T.ones[:, 0:nl], True, False, ["Wc", "ones"], [pk])
+        mm(T.Pf[:, 0:nl], T.Ip[:], T.nm[:, 0:nl], False, False, ["Ip", "nm"], ["Pf"])
+        mm(T.Pd[:, 0:nl], T.In[:], T.sv[:, 0:nl], True, False, ["In", "sv"], ["Pd"])
+        for f in fill1:
+            f()
+        a, b, c = SPLIT[nl]
+        oc, ok = T.Pe[:, 256:256 + M], ["oc0", "oc1"]
+        hv = ((0, 0, a), (1, a, M))
+        ts(T.tm[:, 0:M], T.Pc[:, 0:M], 0.5, OP.is_ge, ["Pc"], ["tm"])
+        for n, lo, hi in hv:
+            tt(T.t2[:, lo:hi], T.tm[:, lo:hi], T.Po[:, lo:hi], OP.mult, ["tm", "Po"], ["t2%d" % n])
+        for n, lo, hi in hv:
+            tt(T.Pe[:, 256 + lo:256 + hi], T.t2[:, lo:hi], T.Po[:, 128 + lo:128 + hi], OP.add, ["t2%d" % n, "Po"], ["oc%d" % n])
+        for n, lo, hi in hv:
+            ts(T.O16[:, lo:hi], T.Pe[:, 256 + lo:256 + hi], float(HALF), OP.add, ["oc%d" % n], ["of%d" % n])
+        parts = ((0, a), (a, a + b), (a + b, M))
+        for n in (0, 2):
+            lo, hi = parts[n]
+            act(T.V[:, 16 * lo:16 * hi], Uw.indirect(T.O16[:, lo:hi]), AF.Copy, UK + ["of%d" % (n // 2)], ["V%d" % n])
+        lo, hi = parts[1]
+        cp(T.V[:, 16 * lo:16 * hi], Uw.indirect(T.O16[:, lo:hi]), UK + ["of1"], ["V1"])
+        for n in (1, 0, 2):
+            lo, hi = parts[n]
+            scan(T.SO[:, 16 * lo:16 * hi], T.lad[:, 0:16 * (hi - lo)], T.V[:, 16 * lo:16 * hi], OP.min, OP.max,
+                 ["lad", "V%d" % n], ["R%d" % n])
+        RK = ["R0", "R1", "R2"]
+        R = T.SO[:, 7:8 * nl:8]
+        mm(T.Pf[:, 0:nl], T.Wz[:], R, False, False, ["Wz"] + RK, ["Pf"])
+        mm(T.Pr[:, 0:nl], T.Wz[:], R, False, False, ["Wz"] + RK, ["Pr"])
+        act(T.tb[:, 0:nl], R, AF.Relu, RK, ["tb"], bias=-1920.0, scale=128.0)
+        ts(T.m[:, 0:M], T.SO[:, 7:8 * nl:16], col(22), OP.is_equal, RK + ["c22"], ["m0"])
+        ts(T.m[:, 128:128 + M], T.SO[:, 15:8 * nl:16], col(23), OP.is_equal, RK + ["c23"], ["m1"])
+        tt(T.y[:, 0:nl:2], T.m[:, 0:M], oc, OP.mult, ["m0"] + ok, ["y0"])
+        tt(T.y[:, 1:nl:2], T.m[:, 128:128 + M], oc, OP.mult, ["m1"] + ok, ["y1"])
+        mm(T.Pf[:, 0:nl], T.Wy[:], T.y[:, 0:nl], False, True, ["Wy", "y0", "y1"], ["Pf"])
+        mm(T.Pr[:, 0:nl], T.Wy[:], T.y[:, 0:nl], False, True, ["Wy", "y0", "y1"], ["Pr"])
+        mm(T.Pq[:, 0:nl], T.Wz[:], R, False, False, ["Wz"] + RK, ["Pq"])
+        mm(T.Pq[:, 0:nl], T.Wy[:], T.y[:, 0:nl], False, True, ["Wy", "y0", "y1"], ["Pq"])
+        mm(T.Pd[:, 0:nl], T.Ip[:], R, False, False, ["Ip"] + RK, ["Pd"])
+        mm(T.Pd[:, 0:nl], T.Ip[:], T.tb[:, 0:nl], False, True, ["Ip", "tb"], ["Pd"])
+        for f in fill2:
+            f()
+        deltas(depth)
+        scan(T.hold[:, 0:nl], T.head[:, 0:nl], T.Pf[:, 0:nl], OP.add, OP.min, ["head", "Pf"], ["hold"])
+        act(T.bia[:, 0:KC], T.hold[:, 15:nl:16], AF.Identity, ["hold"], ["bia"], bias=-3.5, scale=-16.0)
+        for k in range(KC - 1, kv, -1):
+            act(T.junk[:, 256 * k:256 * k + 16 * k], T.Pr[:, 0:16 * k], AF.Tanh, ["Pr", "bia"], ["acc%d" % k],
+                bias=T.bia[:, k:k + 1], scale=16.0, acc=T.acc[:, k:k + 1])
+        act(T.ab[:, 0:nl], T.Pd[:, 0:nl], AF.Relu, ["Pd"], ["ab"], bias=HOLE, scale=-1.0)
+        act(T.dat[:, 0:nl], T.ab[:, 0:nl], AF.Relu, ["ab"], ["dat"], bias=HOLE, scale=-1.0)
+        q = T.hold[:, 15:256:16]
+        ts(T.dn[:], q, 1.0e6, OP.is_ge, ["hold"], ["dn"])
+        tt(T.DL[:, 16:32], q, T.ST[:, 16:32], OP.subtract, ["hold", "cur"], ["Dq"])
+        ts(T.s2[:], q, float(DS), OP.is_ge, ["hold"], ["s2"])
+        ts(T.s1[:], q, float(W), OP.is_ge, ["hold"], ["s1"])
+        tt(T.s4[:], T.dn[:], T.DL[:, 32:48], OP.mult, ["dn", "DL"], ["s4"])
+        tt(T.DL[:, 0:16], T.DL[:, 16:32], T.s2[:], OP.mult, ["Dq", "s2"], ["De"])
+        tt(T.ST[:, 0:16], T.ST[:, 16:32], T.s4[:], OP.subtract, ["cur", "s4"], ["q"])
+        tt(T.eq[:, 0:nl], T.hold[:, 0:nl], T.Pq[:, 0:nl], OP.is_equal, ["hold", "Pq"], ["eq"])
+        for k in range(1, kv + 1):
+            o = 8 * k * (k - 1)
+            ts(T.E[:, o:o + 16 * k], T.Pq[:, 0:16 * k], T.hold[:, 16 * k + 15:16 * k + 16], OP.is_equal,
+               ["Pq", "hold"], ["E%d" % k], -TOL, OP.add)
+            if k == 1:
+                scan(T.SD[:, 0:nl], T.eq[:, 0:nl], T.md[:, 0:nl], OP.max, OP.min, ["eq", "md"], ["SD"])
+        tt(T.s3[:], T.s1[:], T.SD[:, 15:256:16], OP.add, ["s1", "SD"], ["s3"])
+        ne = 8 * kv * (kv + 1)
+        scan(T.Z[:, 16:16 + ne], T.mE[:, 0:ne], T.E[:, 0:ne], OP.min, OP.max,
+             ["mE"] + ["E%d" % k for k in range(1, kv + 1)], ["Z"])
+        if t == 8:
+            hole_flags()
+        zc = 0 if nl == 160 else 2
+        AK = ["acc"] + ["acc%d" % k for k in range(kv + 1, KC)]
+        tt(T.s5[:], T.Z[:, 0:592].indirect(T.zo[:, zc:zc + 1]), T.s3[:], OP.add, ["Z", "Zc", "zo%d" % (zc // 2), "s3"], ["s5"])
+        cp(T.ri[:], T.acc[:], AK, ["ri"])
+        tt(T.s6[:], T.s5[:], T.acc[:], OP.add, ["s5"] + AK, ["s6"])
+        tt(T.WN[:, 0:16], T.s6[:], T.ri[:], OP.is_le, ["s6", "ri"], ["W0"])
+        tt(T.WN[:, 16:32], T.s6[:], T.ri[:], OP.is_le, ["s6", "ri"], ["W1"])
+        tt(T.ee[:], T.WN[:], T.DL[:, 0:32], OP.mult, ["W0", "W1", "Dq", "De"], ["ee"])
+        tt(T.NX[:], T.ST[:, 0:32], T.ee[:], OP.add, ["q", "cur", "ee"], ["NX"])
+        cp(T.co[:], T.NX[:], ["NX"], ["co"])
+
+    def scatter(nl):
+        cp(Uw.indirect(T.co[:, 16:16 + nl // 16]), T.dat[:, 0:nl], ["co", "dat"] + UK, UK)
+
+    def bits(engines):
+        mask = 0
+        for e in engines:
+            mask |= 1 << e
+        return mask
+
+    def exchange(x):
+        land, arr = T["L%d" % x], T.sem["arr%d" % x]
+        up, down, far = (T.cores[(rank + d) % NR] for d in (1, NR - 1, 2))
+        both = [e for e in topo.engines(core, up) if e in topo.engines(core, down)]
+        per = len(both) // 2
+        trs = []
+        for n, (dst, src, out) in enumerate(((up, U[:, 0:BLK], land[:, 0:BLK]),
+                                             (down, U[:, W - DS:W - BLK], land[:, 3 * BLK:4 * BLK]))):
+            ad = topo.addr(dst)
+            trs.append(RemoteDMATransfer(dst_ids=[DstId(rid=ad[0], pnc=ad[1])], dma_engine_mask=bits(both[n * per:(n + 1) * per]),
+                                         remote_sem=arr, src=src, dst=out))
+        add("g", lambda e: e.remote_dma_fused(trs, local_sem=T.sem["near%d" % x]), UK, [], ("near%d" % x, 2 * per))
+        act(T.stg[:, 0:BLK], U[:, BLK:DS], AF.Copy, ["U0"], ["stg0"])
+        act(T.stg[:, BLK:DS], U[:, W - BLK:W], AF.Copy, ["U5"], ["stg1"])
+        ad, nf = topo.addr(far), len(topo.engines(core, far))
+        add("g", lambda e: e.remote_dma(land[:, BLK:3 * BLK], T.stg[:], arr, T.sem["far%d" % x], ad[1], ad[0], topo.mask(core, far)),
+            ["stg0", "stg1"], [], ("far%d" % x, nf))
+        return 2 * per + nf
+
+    def after_exchange(x, total):
+        land = T["L%d" % x]
+        lk = "L%d" % x
+        add("x", None, [], [lk], ("arr%d" % x, total))
+        EX, SI = U[:, W - DS:W], U[:, 0:DS]
+        gl = T.xg[:, 15:96:16]
+        ts(T.xd[:], land[:, 0:DS], HOLE, OP.is_equal, [lk], ["xd"])
+        ts(T.xe[:], land[:, 0:DS], HOLE, OP.not_equal, [lk], ["xe"], HOLE, OP.add)
+        tt(T.xf[:], T.xd[:], T.Pe[:, 96:192], OP.mult, ["xd", "Pe"], ["xf"])
+        tt(T.Pf[:, 0:BLK], land[:, 3 * BLK:4 * BLK], T.Pe[:, 0:BLK], OP.max, [lk, "Pe"], ["Pf"])
+        scan(T.xg[:], T.keep[:, 0:96], T.xf[:], OP.mult, OP.add, ["keep", "xf"], ["xg"])
+        tt(T.Pf[:, BLK:DS], land[:, 2 * BLK:3 * BLK], T.Pe[:, BLK:DS], OP.max, [lk, "Pe", "Pf"], ["pf2"])
+        tt(T.s2[:, 0:6], gl, T.dsl[:, 0:6], OP.mult, ["xg", "dsl"], ["s2"])
+        tt(EX, EX, T.xe[:], OP.min, ["U5", "xe"], ["U5"])
+        tt(T.slf[:, 10:16], T.slf[:, 10:16], T.s2[:, 0:6], OP.add, ["slf", "s2"], ["slf"])
+        tt(SI, SI, T.Pf[:, 0:96], OP.min, ["U0", "Pf", "pf2"], ["U0"])
+        cp(T.sl16[:], T.slf[:], ["slf"], ["sl16"])
+        tt(T.s1[:, 0:6], gl, T.edf[:, 0:6], OP.mult, ["xg", "edf"], ["s1"])
+
+    def start_guests():
+        tt(T.ST[:, 26:32], T.ST[:, 26:32], T.s1[:, 0:6], OP.add, ["cur", "s1"], ["cur"])
+        cp(T.co[:, 10:16], T.ST[:, 26:32], ["cur"], ["co"])
+        gather_args(10, 16, ["A1"])
+        fold_args(OWN, LANES, ["A1"])
+
+    gather_args(0, 10, ["A0", "A1"])
+    mm(T.Ps[:, 0:OWN], T.W0[:], T.A[:, 0:OWN], False, True, ["W0r", "A0", "A1"], ["Ps"])
+    fold_args(0, 160, ["A0", "A1"])
+    scan(T.hold[:, 0:OWN], T.head[:, 0:OWN], T.Ps[:, 0:OWN], OP.add, OP.min, ["head", "Ps"], ["hold"])
+    ts(T.sl16[:, 0:10], T.hold[:, 15:OWN:16], float(HALF), OP.add, ["hold"], ["sl16"])
+    fill0, fill1, fill2 = [], [], []
+    for t in range(1, 9):
+        nl = 160 if t <= 2 else 256
+        step(t, nl, fill0, fill1, fill2)
+        if t == 8:
+            break
+        st = stack_ops(min(t, 8 - t))
+        if t % 2 == 1:
+            gather_args(0, nl // 16, ["A0", "A1"])
+            scatter(nl)
+            list_arg0(T.A, nl, ["A0", "A1"])
+            fold_args(0, nl, ["A0", "A1"])
+            ts(T.sl16[:, 0:nl // 16], T.Ps[:, 0:nl // 16], float(HALF), OP.add, ["Ps"], ["sl16"])
+            fill0, fill1, fill2 = [], st[:6], st[6:]
+            if t == 7:
+                fill1, fill2 = [hole_flags, scatter_out], st
+        else:
+            x = t // 2 - 1
+            scatter(nl)
+            total = exchange(x)
+            gather_args(0, 16, ["A0", "A1"])
+            list_arg0(T.A, 256, ["A0", "A1"])
+            fold_args(0, OWN, ["A0"])
+            for f in st:
+                f()
+            if x == 0:
+                exchange_constants()
+            if x == 2:
+                for k, (a, b) in enumerate(MID):
+                    ts(T.OUT[:, a:b], U[:, a:b], 16.0, OP.is_ge, ["Um"], ["O%d" % k], -33.0, OP.mult)
+            ts(T.slf[:], T.Ps[:, 0:16], float(HALF), OP.add, ["Ps"], ["slf"])
+            if x == 0:
+                ts(T.AE[:], AG[:, 0:WT].indirect(T.ec16[:, 0:6]), float(HALF), OP.subtract, ["AG", "AGr", "ec16"], ["AE"])
+                list_arg0(T.AE, 96, ["AE"])
+                ms(T.acc[:], 0.0, ["acc"] + ["acc%d" % k for k in range(16)])
+                ms(T.OUT[:, W:WT], 0.0, ["Or"])
+            ts(T.xc[:], U[:, W - DS:W], THUNK, OP.is_equal, ["U5"], ["xc"])
+            ts(T.Pe[:, 0:96], U[:, 0:DS], HOLE, OP.not_equal, ["U0"], ["Pe"], 64.0, OP.mult)
+            tt(T.Pe[:, 96:192], T.xc[:], T.am[:], OP.mult, ["xc", "am"], ["Pe"])
+            if x == 0:
+                ts(T.slE[:, 0:6], T.Ps[:, 0:6], float(HALF), OP.add, ["Ps"], ["slE"])
+            tt(T.dsl[:, 0:6], T.slE[:, 0:6], T.slf[:, 10:16], OP.subtract, ["slE", "slf"], ["dsl"])
+            after_exchange(x, total)
+            fill0, fill1, fill2 = [start_guests], [], []
+            if x == 2:
+                for k, (a, b) in enumerate(MID):
+                    dma("g", T.OUT[:, a:b], U[:, a:b], ["Um", "L2", "O%d" % k], ["O%d" % k], True)
+                fill2 = [unfold_ends]
+
+    scatter_out()
+    dma("y", T.yv[:, 0:HALF], T.OUT[:, 0:HALF], OK, ["yv0"])
+    dma("s", T.yv[:, HALF:W], T.OUT[:, HALF:W], OK, ["yv1"])
+    mm(T.Pe[:, 0:16], T.Wr[:], T.NX[:, 0:16], True, True, ["Wr", "NX"], ["Pe"])
+    ts(T.s1[:], T.Pe[:, 0:16], float(W), OP.is_ge, ["Pe"], ["s1"], -8192.0, OP.mult)
+    tt(T.s2[:], T.s1[:], T.Pe[:, 0:16], OP.add, ["s1", "Pe"], ["s2"])
+    ts(T.yo[:], T.s2[:], -1.0, OP.max, ["s2"], ["yo"])
+    dma("y", T.ya[:], T.yo[:], ["yo"], ["ya"])
+    return ops
+
+
+def emit(g, T, ops):
+    eng = {"v": g.vector, "s": g.scalar, "t": g.tensor, "g": g, "y": g.sync}
+    writer, readers, known, clock, waits = {}, {}, {q: {} for q in eng}, [], []
+    lane, pos, count, nd = [], [], {}, [0]
+    for n, (q, fn, rd, wr, kind) in enumerate(ops):
+        if kind == "c":
+            ln = "q" + q
+        elif kind == "d":
+            ln = "d%d" % nd[0]
+            nd[0] += 1
+        else:
+            ln = kind[0]
+        count[ln] = count.get(ln, 0) + 1
+        lane.append(ln)
+        pos.append(count[ln])
+        deps = set()
+        for k in rd:
+            if k in writer:
+                deps.add(writer[k])
+            if k[0] == "P":
+                deps.update(r for r in readers.get(k, []) if ops[r][0] != q)
+        for k in wr:
+            if k in writer:
+                deps.add(writer[k])
+            deps.update(readers.get(k, []))
+        if q == "t":
+            deps = set(d for d in deps if ops[d][0] != "t")
+        need = []
+        if q != "x":
+            kn = known[q]
+            for d in sorted(deps, reverse=True):
+                if kn.get(lane[d], 0) < pos[d]:
+                    need.append(d)
+                    for l, p in clock[d].items():
+                        kn[l] = max(kn.get(l, 0), p)
+            ck = dict(kn)
+        else:
+            ck = {}
+        ck[ln] = pos[n]
+        clock.append(ck)
+        waits.append(need)
+        for k in rd:
+            readers.setdefault(k, []).append(n)
+        for k in wr:
+            writer[k] = n
+            readers[k] = []
+    signal = set(d for need in waits for d in need)
+    value, total = {}, {}
+    for n, (q, fn, rd, wr, kind) in enumerate(ops):
+        ln = lane[n]
+        if kind == "c":
+            if n in signal:
+                total[ln] = total.get(ln, 0) + 1
+        elif kind == "d":
+            total[ln] = 16
+        else:
+            total[ln] = kind[1]
+        value[n] = total.get(ln, 0)
+    for n, (q, fn, rd, wr, kind) in enumerate(ops):
+        if q == "x":
+            continue
+        e = eng[q]
+        for d in waits[n]:
+            e.wait_ge(T.sem[lane[d]], value[d])
+        ins = fn(e)
+        if kind == "d":
+            ins.then_inc(T.sem[lane[n]], 16)
+        elif kind == "c" and n in signal:
+            ins.then_inc(T.sem[lane[n]], 1)
+    for ln in sorted(total):
+        g.wait_ge(T.sem[ln], total[ln])
+
+
+def rank_program(g, core, T, topo):
+    if T.rank_of(core) is None:
+        return
+    emit(g, T, build(core, T, topo))

@@ -7,9 +7,11 @@ W, OWN, BLK, DS, LANES, NR = 3072, 160, 48, 96, 256, 4
 WT = W + LANES
 HOLE, THUNK = 31.0, 32.0
 HALF = 1536
-TOL = 2.0 ** -10
-BIG = 2.0 ** 23
-KV = {160: 4, 256: 8}
+TOL = 3.0 * 2.0 ** -13
+BIG = 2.0 ** 27
+X = 16.0
+KV = {160: 4, 256: 9}
+NE = 720
 SPLIT = {160: (34, 30, 16), 256: (56, 48, 24)}
 
 F32, BF, F16, I32, U16 = "float32", "bfloat16", "float16", "int32", "uint16"
@@ -25,21 +27,21 @@ SCRATCH = {
     "pi": _sb(8, I32), "pc": _sb(32, F32), "io_c": _sb(144, BF), "io_s": _sb(256, BF), "io_g": _sb(128, BF),
     "io_h": _sb(128, BF), "io_t": _sb(896, BF), "io_k": _sb(96, F32),
     "Wsl": _sb(144, F16), "Wd": _sb(144, F16), "Wf": _sb(144, F16), "Wy": _sb(128, F16), "W0": _sb(128, F16), "Wz": _sb(128, BF),
-    "Wlo": _sb(128, BF), "Whi": _sb(128, BF), "Wc": _sb(128, BF), "Ip": _sb(128, BF), "In": _sb(128, BF),
+    "Wlo": _sb(128, BF), "Whi": _sb(128, BF), "Wc": _sb(128, BF), "Wc4": _sb(128, BF), "Ip": _sb(128, BF), "In": _sb(128, BF),
     "Wr": _sb(128, F32), "ones": _sb(256, BF), "lad": _sb(896, BF), "nm": _sb(256, BF), "keep": _sb(256, BF),
-    "head": _sb(256, BF), "md": _sb(256, BF), "am": _sb(96, BF), "mE": _sb(576, BF), "zo": _sb(4, U16), "hol": _sb(160, BF),
+    "head": _sb(256, BF), "md": _sb(256, BF), "am": _sb(96, BF), "mE": _sb(NE, BF), "zo": _sb(4, U16), "hol": _sb(160, BF),
     "ecf": _sb(16, F32), "ec16": _sb(16, U16), "edf": _sb(16, F32), "slE": _sb(16, F32), "slf": _sb(16, F32), "dsl": _sb(16, F32),
     "A": _sb(256, F16), "AE": _sb(96, F16), "sl16": _sb(16, U16), "ind": _sb(256, BF), "sv": _sb(256, BF),
     "tm": _sb(128, F32), "t2": _sb(128, F32), "O16": _sb(128, U16), "V": _sb(2048, BF), "SO": _sb(2048, BF),
     "m": _sb(256, BF), "y": _sb(256, F16), "tb": _sb(256, BF), "ab": _sb(256, BF), "dat": _sb(256, BF), "tn": _sb(256, BF),
-    "hold": _sb(256, F32), "bia": _sb(16, F32), "eq": _sb(256, BF),
-    "SD": _sb(256, BF), "E": _sb(576, BF), "Z": _sb(592, BF), "junk": _sb(4096, BF), "acc": _sb(16, F32),
+    "hold": _sb(256, F32), "eq": _sb(256, BF),
+    "SD": _sb(256, BF), "E": _sb(NE, BF), "Z": _sb(NE + 16, BF), "junk": _sb(4096, BF), "acc": _sb(16, F32),
     "ST": _sb(112, F32), "DL": _sb(112, F32), "dn": _sb(16, F32), "s1": _sb(16, F32), "s2": _sb(16, F32),
     "s3": _sb(16, F32), "s4": _sb(16, F32), "s5": _sb(16, F32), "s6": _sb(16, F32), "ri": _sb(16, I32),
-    "WN": _sb(32, F32), "ee": _sb(32, F32), "NX": _sb(32, F32),
+    "XB": _sb(64, F32), "DB": _sb(64, F32), "NX": _sb(64, F32),
     "co": _sb(32, U16), "ent": _sb(16, F32), "pa": _sb(64, F32), "pb": _sb(64, F32),
     "L0": _sb(192, BF), "L1": _sb(192, BF), "L2": _sb(192, BF), "stg": _sb(96, BF),
-    "xc": _sb(96, BF), "xd": _sb(96, BF), "xe": _sb(96, BF), "xf": _sb(96, BF), "xg": _sb(96, BF),
+    "xc": _sb(96, BF), "xd": _sb(96, BF), "xf": _sb(96, BF), "xg": _sb(96, BF),
     "yo": _sb(16, F32),
     "Pq": ("psum", [128, 512], F32), "Pr": ("psum", [128, 512], F32), "Pc": ("psum", [128, 512], F32),
     "Po": ("psum", [128, 512], F32), "Ps": ("psum", [128, 512], F32), "Pd": ("psum", [128, 512], F32),
@@ -96,12 +98,14 @@ def build(core, T, topo):
     Uw = U[:, 0:WT]
     UK = ["U0", "U1", "U2", "U3", "U4", "U5", "Ur", "Um"]
     OK = ["O0", "O1", "O2", "O3", "Or"]
+    SL = ["slo", "slg"]
     MID = ((DS, HALF), (HALF, W - DS))
+    QB = ((T.Pf, "Pf"), (T.Pq, "Pq"), (T.Pr, "Pr"))
 
     def col(j):
         return pc[:, j:j + 1]
 
-    dma("y", T.rti[:, 0:10], T.rts[:], [], ["rti"])
+    dma("s", T.rti[:, 0:10], T.rts[:], [], ["rti"])
     dma("y", T.VR[:, 0:HALF], T.vals[:, 0:HALF], [], ["VR0"])
     dma("y", T.VR[:, HALF:W], T.vals[:, HALF:W], [], ["VR1"])
     dma("y", AG[:, 0:W], T.ag[:], [], ["AG"])
@@ -111,7 +115,7 @@ def build(core, T, topo):
 
     iota(T.pi[:, 0:1], [[0, 1]], 0, 1, ["pi0"], False)
     iota(T.io_c[:], [[1, 144]], 0, 0, ["io_c"])
-    iota(T.io_k[:], [[0, 6], [16, 16]], 0, 0, ["io_k"])
+    iota(T.io_k[:], [[0, 6], [256, 16]], 0, 0, ["io_k"])
     iota(T.io_h[:], [[1, 16], [0, 8]], 0, 0, ["io_h"])
     iota(T.io_g[:], [[1, 8], [0, 16]], 0, 0, ["io_g"])
     iota(T.io_s[:], [[0, 16], [1, 16]], 0, 0, ["io_s"])
@@ -128,56 +132,60 @@ def build(core, T, topo):
     P, I, G, TT = col(0), col(1), col(2), col(3)
     c0 = ["c0"]
     ms(T.Z[:, 0:16], -TOL, ["Zc"])
-    ms(T.Z[:, 16:592], 0.0, ["Z"])
+    ms(T.Z[:, 16:NE + 16], 0.0, ["Z"])
     ts(col(6), I, 0.0, OP.is_equal, c0, ["c6"])
     ts(col(9), I, 8.0, OP.is_ge, c0, ["c9"])
-    ts(col(13), I, 1.0, OP.is_equal, c0, ["c13"], 8192.0, OP.mult)
+    ts(col(13), I, 1.0, OP.is_equal, c0, ["c13"], 8192.0 * X, OP.mult)
+    ts(col(28), P, 2.0, OP.is_equal, c0, ["c28"], 4.0, OP.mult)
     aff(7, P, c0, 1.0, 15.0)
     aff(4, G, c0, 16.0, 15.0)
+    aff(29, I, c0, X, W * X)
     aff(11, G, c0, 2.0, 0.0)
     aff(12, G, c0, 2.0, 1.0)
     aff(5, I, ["c0", "c7"], -2.0, col(7))
     aff(8, TT, ["c0", "c4"], -1.0, col(4))
     aff(10, col(9), ["c9"], -2.0, 1.0)
-    aff(14, col(6), ["c6", "c13"], -131072.0, col(13))
+    aff(14, col(6), ["c6", "c13"], -131072.0 * X, col(13))
     aff(15, col(13), ["c13"], 192.0 / 8192.0, 0.0)
     aff(18, col(6), ["c6"], -1.875, 2.0)
     aff(19, col(6), ["c6"], 15.0, 16.0)
     aff(20, TT, c0, 2.0, 18.0)
     aff(25, I, c0, 8.0, 8.0)
-    aff(17, col(6), ["c6", "c15"], 491520.0, col(15))
+    aff(17, col(6), ["c6", "c15"], 491520.0 * X, col(15))
     aff(21, col(6), ["c6", "c20"], 13.125, col(20))
     aff(26, col(25), ["c25", "c0"], I, 0.0)
+    aff(30, col(28), ["c28", "c17"], 1.0, col(17))
     aff(22, col(9), ["c9", "c21"], -100.0, col(21))
     aff(16, col(21), ["c21"], 1.0, -100.0)
     aff(24, I, c0, -1.0, 15.0)
     aff(23, col(9), ["c9", "c16"], 100.0, col(16))
     act(T.keep[:], T.io_s[:], AF.Tanh, ["io_s"], ["keep"], scale=20.0)
     ms(T.SD[:], 0.0, ["SD"])
-    ms(T.hold[:, OWN:LANES], 1.0e5, ["hold"])
+    ms(T.DB[:], 0.0, ["DB0", "Dq", "De"])
+    ms(T.hold[:, OWN:LANES], 1.0e5 * X, ["hold"])
     ms(T.mE[:], 2.0, ["mE"])
     ts(T.Wr[:], T.io_c[:, 0:128], col(5), OP.is_equal, ["io_c", "c5"], ["Wr"])
-    ts(T.ST[:, 16:112], T.io_k[:], I, OP.add, ["io_k", "c0"], ["cur", "S"], float(W), OP.add)
+    ts(T.ST[:, 16:112], T.io_k[:], col(29), OP.add, ["io_k", "c29"], ["cur", "S"])
     ms(T.mE[:, 0:17:16], -1.0, ["mE"])
     ts(T.Wsl[:], T.io_c[:], col(7), OP.is_equal, ["io_c", "c6", "c7"], ["Wsl"], col(6), OP.mult)
     ts(T.Ip[:], T.io_c[:, 0:128], P, OP.is_equal, ["io_c", "c0"], ["Ip"])
     ms(T.mE[:, 48:97:48], -1.0, ["mE"])
     ts(T.In[:], T.io_c[:, 0:128], P, OP.is_equal, ["io_c", "c0"], ["In"], -1.0, OP.mult)
-    cp(T.rtf[:, 0:10], T.rti[:, 0:10], ["rti"], ["rtf"])
+    ts(T.rtf[:, 0:10], T.rti[:, 0:10], X, OP.mult, ["rti"], ["rtf"])
     mm(T.Pe[:, 0:10], T.Wr[:], T.rtf[:, 0:10], True, True, ["Wr", "rtf"], ["Pe"])
     ts(T.Wd[:], T.io_c[:], col(8), OP.is_equal, ["io_c", "c8", "c10"], ["Wd"], col(10), OP.mult)
     ts(T.Wf[:], T.io_c[:], col(8), OP.is_equal, ["io_c", "c8", "c9"], ["Wf"], col(9), OP.mult)
     ts(T.Wlo[:], T.io_h[:], col(11), OP.is_equal, ["io_h", "c11"], ["Wlo"])
     ts(T.Whi[:], T.io_h[:], col(12), OP.is_equal, ["io_h", "c12"], ["Whi"])
-    ts(T.Wy[:], T.io_g[:], G, OP.is_equal, ["io_g", "c0"], ["Wy"])
+    ts(T.Wy[:], T.io_g[:], G, OP.is_equal, ["io_g", "c0"], ["Wy"], X, OP.mult)
     ts(T.Wz[:], T.io_g[:], G, OP.is_equal, ["io_g", "c0", "c14"], ["Wz"], col(14), OP.mult)
     cp(T.ST[:, 16:26], T.Pe[:, 0:10], ["Pe"], ["cur"])
     ts(T.Wc[:], T.ones[:, 0:128], col(17), OP.mult, ["ones", "c17"], ["Wc"])
-    cp(T.co[:, 0:16], T.ST[:, 16:32], ["cur"], ["co"])
+    ts(T.co[:, 0:16], T.ST[:, 16:32], 1.0 / X, OP.mult, ["cur"], ["co"])
+    ts(T.Wc4[:], T.ones[:, 0:128], col(30), OP.mult, ["ones", "c30"], ["Wc4"])
     ts(T.nm[:], T.io_s[:], I, OP.not_equal, ["io_s", "c0"], ["nm"], BIG, OP.mult)
     ts(T.md[:], T.io_s[:], I, OP.is_gt, ["io_s", "c0"], ["md"])
     ts(T.W0[:], T.io_g[:], G, OP.is_equal, ["io_g", "c0", "c6"], ["W0r"], col(6), OP.mult)
-    mm(T.Ps[:, 0:OWN], T.Ip[:], T.nm[:, 0:OWN], True, False, ["Ip", "nm"], ["Ps"])
 
     def ends(n, nl):
         ts(col(27), I, KV[nl] + 0.5, OP.is_lt, ["c0", "c26"], ["c27"], col(26), OP.mult)
@@ -195,9 +203,9 @@ def build(core, T, topo):
     ms(T.lad[:, 0::8], 0.0, ["lad"])
 
     def exchange_constants():
-        ts(T.ecf[:, 0:6], T.io_k[:, 0:6], I, OP.subtract, ["io_k", "c0"], ["ecf"], float(W - DS + 15), OP.add)
+        ts(T.ecf[:, 0:6], T.io_k[:, 0:6], col(29), OP.subtract, ["io_k", "c29"], ["ecf"], (2 * W - DS + 15) * X, OP.add)
         ts(T.am[:], T.io_s[:, 0:96], col(24), OP.is_equal, ["io_s", "c24"], ["am"])
-        cp(T.ec16[:, 0:6], T.ecf[:, 0:6], ["ecf"], ["ec16"])
+        ts(T.ec16[:, 0:6], T.ecf[:, 0:6], 1.0 / X, OP.mult, ["ecf"], ["ec16"])
         tt(T.edf[:, 0:6], T.ecf[:, 0:6], T.ST[:, 106:112], OP.subtract, ["ecf", "S"], ["edf"])
         ends(1, 256)
         for k in range(5, KV[256] + 1):
@@ -211,6 +219,16 @@ def build(core, T, topo):
         for r in range(16):
             mm(T.Ps[:, 0:nl // 16], T.Wsl[:, 15 - r:143 - r], src[:, r:nl:16], r == 0, r == 15, ["Wsl"] + key, ["Ps"])
 
+    def spread_arg0():
+        mm(T.Ps[:, 0:OWN], T.Ip[:], T.nm[:, 0:OWN], True, False, ["Ip", "nm"], ["Ps"])
+        mm(T.Ps[:, 0:OWN], T.W0[:], T.A[:, 0:OWN], False, True, ["W0r", "A0", "A1"], ["Ps"])
+
+    def hold_arg0():
+        scan(T.hold[:, 0:OWN], T.head[:, 0:OWN], T.Ps[:, 0:OWN], OP.add, OP.min, ["head", "Ps"], ["hold"])
+
+    def held_list():
+        ts(T.sl16[:, 0:10], T.hold[:, 15:OWN:16], float(HALF), OP.add, ["hold"], SL)
+
     def fold_args(l0, l1, key):
         for n, wt, wk in ((0, T.Wd, "Wd"), (128, T.Wf, "Wf")):
             for h in range(2):
@@ -222,8 +240,8 @@ def build(core, T, topo):
         tt(T.DL[:, 32:32 + n], T.ST[:, 16:16 + n], T.ST[:, 32:32 + n], OP.subtract, ["cur", "S"], ["DL"])
 
     def stack_ops(depth):
-        o = [lambda: ts(T.ent[:], T.ee[:, 0:16], 0.0, OP.not_equal, ["ee"], ["ent"]),
-             lambda: cp(T.ST[:, 16:32], T.NX[:, 0:16], ["NX"], ["cur"])]
+        o = [lambda: tt(T.ent[:], T.NX[:, 1:32:2], T.XB[:, 1:32:2], OP.not_equal, ["NX", "q"], ["ent"]),
+             lambda: cp(T.ST[:, 16:32], T.NX[:, 1:32:2], ["NX"], ["cur"])]
         for d in range(1, depth + 1):
             o.append(lambda d=d: tt(T.pb[:, 16 * d - 16:16 * d], T.dn[:], T.DL[:, 16 * d + 32:16 * d + 48], OP.mult,
                                     ["dn", "DL"], ["pb%d" % d]))
@@ -252,25 +270,26 @@ def build(core, T, topo):
         M, KC, kv = nl // 2, nl // 16, KV[nl]
         depth = min(t, 8 - t)
         kh = (KC + 2) // 4 * 2
-        ts(T.ind[:, 0:16 * kh], Uw.indirect(T.sl16[:, 0:kh]), 8.0, OP.is_ge, UK + ["sl16"], ["ind0"], 0.5, OP.subtract)
-        act(T.ind[:, 16 * kh:nl], Uw.indirect(T.sl16[:, kh:KC]), AF.Sign, UK + ["sl16"], ["ind1"], bias=-7.5)
-        act(T.sv[:, 0:nl], Uw.indirect(T.sl16[:, 0:KC]), AF.Copy, UK + ["sl16"], ["sv"])
+        (v0, v1, vk), (s0, s1, sk) = ((10, 16, ["slg"]), (0, 10, ["slo"])) if fill0 else ((0, kh, SL), (kh, KC, SL))
+        act(T.ind[:, 16 * s0:16 * s1], Uw.indirect(T.sl16[:, s0:s1]), AF.Sign, UK + sk, ["ind1"], bias=-7.5)
+        ts(T.ind[:, 16 * v0:16 * v1], Uw.indirect(T.sl16[:, v0:v1]), 8.0, OP.is_ge, UK + vk, ["ind0"], 0.5, OP.subtract)
+        act(T.sv[:, 0:nl], Uw.indirect(T.sl16[:, 0:KC]), AF.Copy, UK + SL, ["sv"])
         mm(T.Pc[:, 0:M], T.Wlo[:], T.ind[:, 0:nl:2], True, False, ["Wlo", "ind0", "ind1"], ["Pc"])
         mm(T.Pc[:, 0:M], T.Whi[:], T.ind[:, 1:nl:2], False, True, ["Whi", "ind0", "ind1"], ["Pc"])
         for f in fill0:
             f()
-        for pq, pk in ((T.Pf, "Pf"), (T.Pq, "Pq"), (T.Pr, "Pr")):
-            mm(pq[:, 0:nl], T.Wc[:], T.ones[:, 0:nl], True, False, ["Wc", "ones"], [pk])
+        for pq, pk in QB:
+            mm(pq[:, 0:nl], T.Wc4[:] if pk == "Pr" else T.Wc[:], T.ones[:, 0:nl], True, False, ["Wc", "Wc4", "ones"], [pk])
         mm(T.Pf[:, 0:nl], T.Ip[:], T.nm[:, 0:nl], False, False, ["Ip", "nm"], ["Pf"])
         mm(T.Pd[:, 0:nl], T.In[:], T.sv[:, 0:nl], True, False, ["In", "sv"], ["Pd"])
         for f in fill1:
             f()
         a, b, c = SPLIT[nl]
-        oc, ok = T.Pe[:, 256:256 + M], ["oc0", "oc1"]
         hv = ((0, 0, a), (1, a, M))
-        ts(T.tm[:, 0:M], T.Pc[:, 0:M], 0.5, OP.is_ge, ["Pc"], ["tm"])
         for n, lo, hi in hv:
-            tt(T.t2[:, lo:hi], T.tm[:, lo:hi], T.Po[:, lo:hi], OP.mult, ["tm", "Po"], ["t2%d" % n])
+            ts(T.tm[:, lo:hi], T.Pc[:, lo:hi], 0.5, OP.is_ge, ["Pc"], ["tm%d" % n])
+        for n, lo, hi in hv:
+            tt(T.t2[:, lo:hi], T.tm[:, lo:hi], T.Po[:, lo:hi], OP.mult, ["tm%d" % n, "Po"], ["t2%d" % n])
         for n, lo, hi in hv:
             tt(T.Pe[:, 256 + lo:256 + hi], T.t2[:, lo:hi], T.Po[:, 128 + lo:128 + hi], OP.add, ["t2%d" % n, "Po"], ["oc%d" % n])
         for n, lo, hi in hv:
@@ -280,67 +299,70 @@ def build(core, T, topo):
             lo, hi = parts[n]
             act(T.V[:, 16 * lo:16 * hi], Uw.indirect(T.O16[:, lo:hi]), AF.Copy, UK + ["of%d" % (n // 2)], ["V%d" % n])
         lo, hi = parts[1]
+        cp(T.XB[:, 33:64:2], T.ST[:, 16:32], ["cur"], ["xc1"])
         cp(T.V[:, 16 * lo:16 * hi], Uw.indirect(T.O16[:, lo:hi]), UK + ["of1"], ["V1"])
         for n in (1, 0, 2):
             lo, hi = parts[n]
             scan(T.SO[:, 16 * lo:16 * hi], T.lad[:, 0:16 * (hi - lo)], T.V[:, 16 * lo:16 * hi], OP.min, OP.max,
                  ["lad", "V%d" % n], ["R%d" % n])
+            for pq, pk in QB:
+                mm(pq[:, 2 * lo:2 * hi], T.Wz[:], T.SO[:, 16 * lo + 7:16 * hi:8], False, False, ["Wz", "R%d" % n], [pk])
         RK = ["R0", "R1", "R2"]
         R = T.SO[:, 7:8 * nl:8]
-        mm(T.Pf[:, 0:nl], T.Wz[:], R, False, False, ["Wz"] + RK, ["Pf"])
-        mm(T.Pr[:, 0:nl], T.Wz[:], R, False, False, ["Wz"] + RK, ["Pr"])
-        act(T.tb[:, 0:nl], R, AF.Relu, RK, ["tb"], bias=-1920.0, scale=128.0)
-        ts(T.m[:, 0:M], T.SO[:, 7:8 * nl:16], col(22), OP.is_equal, RK + ["c22"], ["m0"])
-        ts(T.m[:, 128:128 + M], T.SO[:, 15:8 * nl:16], col(23), OP.is_equal, RK + ["c23"], ["m1"])
-        tt(T.y[:, 0:nl:2], T.m[:, 0:M], oc, OP.mult, ["m0"] + ok, ["y0"])
-        tt(T.y[:, 1:nl:2], T.m[:, 128:128 + M], oc, OP.mult, ["m1"] + ok, ["y1"])
-        mm(T.Pf[:, 0:nl], T.Wy[:], T.y[:, 0:nl], False, True, ["Wy", "y0", "y1"], ["Pf"])
-        mm(T.Pr[:, 0:nl], T.Wy[:], T.y[:, 0:nl], False, True, ["Wy", "y0", "y1"], ["Pr"])
-        mm(T.Pq[:, 0:nl], T.Wz[:], R, False, False, ["Wz"] + RK, ["Pq"])
-        mm(T.Pq[:, 0:nl], T.Wy[:], T.y[:, 0:nl], False, True, ["Wy", "y0", "y1"], ["Pq"])
         mm(T.Pd[:, 0:nl], T.Ip[:], R, False, False, ["Ip"] + RK, ["Pd"])
-        mm(T.Pd[:, 0:nl], T.Ip[:], T.tb[:, 0:nl], False, True, ["Ip", "tb"], ["Pd"])
+        act(T.tb[:, 0:nl], R, AF.Relu, RK, ["tb"], bias=-1920.0, scale=128.0)
         for f in fill2:
             f()
-        deltas(depth)
+        ts(T.m[:, 0:M], T.SO[:, 7:8 * nl:16], col(22), OP.is_equal, RK + ["c22"], ["m0"])
+        ts(T.m[:, 128:128 + M], T.SO[:, 15:8 * nl:16], col(23), OP.is_equal, RK + ["c23"], ["m1"])
+        yv = ((0, 0, M // 2), (1, M // 2, M)) if nl == LANES else ((1, 0, M),)
+        for n, lo, hi in yv:
+            for h in range(2):
+                tt(T.y[:, 2 * lo + h:2 * hi:2], T.m[:, 128 * h + lo:128 * h + hi], T.Pe[:, 256 + lo:256 + hi], OP.mult,
+                   ["m%d" % h, "oc0", "oc1"], ["y%d%d" % (n, h)])
+            mm(T.Pf[:, 2 * lo:2 * hi], T.Wy[:], T.y[:, 2 * lo:2 * hi], False, n == 1, ["Wy", "y%d0" % n, "y%d1" % n], ["Pf"])
+        for pq, pk in QB[1:]:
+            mm(pq[:, 0:nl], T.Wy[:], T.y[:, 0:nl], False, True, ["Wy", "y00", "y01", "y10", "y11"], [pk])
+        mm(T.Pd[:, 0:nl], T.Ip[:], T.tb[:, 0:nl], False, True, ["Ip", "tb"], ["Pd"])
+        if t == 7:
+            unfold_ends()
+        if t == 8:
+            hole_flags()
         scan(T.hold[:, 0:nl], T.head[:, 0:nl], T.Pf[:, 0:nl], OP.add, OP.min, ["head", "Pf"], ["hold"])
-        act(T.bia[:, 0:KC], T.hold[:, 15:nl:16], AF.Identity, ["hold"], ["bia"], bias=-3.5, scale=-16.0)
+        deltas(depth)
         for k in range(KC - 1, kv, -1):
-            act(T.junk[:, 256 * k:256 * k + 16 * k], T.Pr[:, 0:16 * k], AF.Tanh, ["Pr", "bia"], ["acc%d" % k],
-                bias=T.bia[:, k:k + 1], scale=16.0, acc=T.acc[:, k:k + 1])
+            act(T.junk[:, 256 * k:256 * k + 16 * k], T.Pr[:, 0:16 * k], AF.Tanh, ["Pr", "hold"], ["acc%d" % k],
+                bias=T.hold[:, 16 * k + 15:16 * k + 16], scale=-1.0, acc=T.acc[:, k:k + 1])
         act(T.ab[:, 0:nl], T.Pd[:, 0:nl], AF.Relu, ["Pd"], ["ab"], bias=HOLE, scale=-1.0)
         act(T.dat[:, 0:nl], T.ab[:, 0:nl], AF.Relu, ["ab"], ["dat"], bias=HOLE, scale=-1.0)
         q = T.hold[:, 15:256:16]
-        ts(T.dn[:], q, 1.0e6, OP.is_ge, ["hold"], ["dn"])
-        tt(T.DL[:, 16:32], q, T.ST[:, 16:32], OP.subtract, ["hold", "cur"], ["Dq"])
-        ts(T.s2[:], q, float(DS), OP.is_ge, ["hold"], ["s2"])
-        ts(T.s1[:], q, float(W), OP.is_ge, ["hold"], ["s1"])
-        tt(T.s4[:], T.dn[:], T.DL[:, 32:48], OP.mult, ["dn", "DL"], ["s4"])
-        tt(T.DL[:, 0:16], T.DL[:, 16:32], T.s2[:], OP.mult, ["Dq", "s2"], ["De"])
-        tt(T.ST[:, 0:16], T.ST[:, 16:32], T.s4[:], OP.subtract, ["cur", "s4"], ["q"])
         tt(T.eq[:, 0:nl], T.hold[:, 0:nl], T.Pq[:, 0:nl], OP.is_equal, ["hold", "Pq"], ["eq"])
         for k in range(1, kv + 1):
             o = 8 * k * (k - 1)
             ts(T.E[:, o:o + 16 * k], T.Pq[:, 0:16 * k], T.hold[:, 16 * k + 15:16 * k + 16], OP.is_equal,
                ["Pq", "hold"], ["E%d" % k], -TOL, OP.add)
-            if k == 1:
+            if k == 2:
                 scan(T.SD[:, 0:nl], T.eq[:, 0:nl], T.md[:, 0:nl], OP.max, OP.min, ["eq", "md"], ["SD"])
-        tt(T.s3[:], T.s1[:], T.SD[:, 15:256:16], OP.add, ["s1", "SD"], ["s3"])
+        ts(T.s1[:], q, W * X, OP.is_ge, ["hold"], ["s1"])
+        ts(T.dn[:], q, 1.0e6 * X, OP.is_ge, ["hold"], ["dn"])
         ne = 8 * kv * (kv + 1)
         scan(T.Z[:, 16:16 + ne], T.mE[:, 0:ne], T.E[:, 0:ne], OP.min, OP.max,
              ["mE"] + ["E%d" % k for k in range(1, kv + 1)], ["Z"])
-        if t == 8:
-            hole_flags()
+        tt(T.s3[:], T.s1[:], T.SD[:, 15:256:16], OP.add, ["s1", "SD"], ["s3"])
+        tt(T.DB[:, 33:64:2], q, T.ST[:, 16:32], OP.subtract, ["hold", "cur"], ["Dq"])
+        ts(T.s2[:], q, DS * X, OP.is_ge, ["hold"], ["s2"])
         zc = 0 if nl == 160 else 2
         AK = ["acc"] + ["acc%d" % k for k in range(kv + 1, KC)]
-        tt(T.s5[:], T.Z[:, 0:592].indirect(T.zo[:, zc:zc + 1]), T.s3[:], OP.add, ["Z", "Zc", "zo%d" % (zc // 2), "s3"], ["s5"])
+        tt(T.s5[:], T.Z[:, 0:NE + 16].indirect(T.zo[:, zc:zc + 1]), T.s3[:], OP.add, ["Z", "Zc", "zo%d" % (zc // 2), "s3"], ["s5"])
+        tt(T.s4[:], T.dn[:], T.DL[:, 32:48], OP.mult, ["dn", "DL"], ["s4"])
         cp(T.ri[:], T.acc[:], AK, ["ri"])
         tt(T.s6[:], T.s5[:], T.acc[:], OP.add, ["s5"] + AK, ["s6"])
-        tt(T.WN[:, 0:16], T.s6[:], T.ri[:], OP.is_le, ["s6", "ri"], ["W0"])
-        tt(T.WN[:, 16:32], T.s6[:], T.ri[:], OP.is_le, ["s6", "ri"], ["W1"])
-        tt(T.ee[:], T.WN[:], T.DL[:, 0:32], OP.mult, ["W0", "W1", "Dq", "De"], ["ee"])
-        tt(T.NX[:], T.ST[:, 0:32], T.ee[:], OP.add, ["q", "cur", "ee"], ["NX"])
-        cp(T.co[:], T.NX[:], ["NX"], ["co"])
+        tt(T.DB[:, 1:32:2], T.DB[:, 33:64:2], T.s2[:], OP.mult, ["Dq", "s2"], ["De"])
+        tt(T.XB[:, 1:32:2], T.ST[:, 16:32], T.s4[:], OP.subtract, ["cur", "s4"], ["q"])
+        tt(T.XB[:, 0:32:2], T.s6[:], T.ri[:], OP.is_le, ["s6", "ri"], ["W0"])
+        tt(T.XB[:, 32:64:2], T.s6[:], T.ri[:], OP.is_le, ["s6", "ri"], ["W1"])
+        scan(T.NX[:], T.DB[:], T.XB[:], OP.mult, OP.add, ["DB0", "Dq", "De", "q", "xc1", "W0", "W1"], ["NX"])
+        ts(T.co[:], T.NX[:, 1:64:2], 1.0 / X, OP.mult, ["NX"], ["co"])
 
     def scatter(nl):
         cp(Uw.indirect(T.co[:, 16:16 + nl // 16]), T.dat[:, 0:nl], ["co", "dat"] + UK, UK)
@@ -376,30 +398,30 @@ def build(core, T, topo):
         add("x", None, [], [lk], ("arr%d" % x, total))
         EX, SI = U[:, W - DS:W], U[:, 0:DS]
         gl = T.xg[:, 15:96:16]
+        ts(T.Pf[:, 96:192], land[:, 0:DS], HOLE, OP.not_equal, [lk], ["Pf"], HOLE, OP.add)
         ts(T.xd[:], land[:, 0:DS], HOLE, OP.is_equal, [lk], ["xd"])
-        ts(T.xe[:], land[:, 0:DS], HOLE, OP.not_equal, [lk], ["xe"], HOLE, OP.add)
+        tt(T.Pf[:, 0:BLK], land[:, 3 * BLK:4 * BLK], T.Pe[:, 0:BLK], OP.max, [lk, "Pe"], ["pf1"])
+        tt(T.Pf[:, BLK:DS], land[:, 2 * BLK:3 * BLK], T.Pe[:, BLK:DS], OP.max, [lk, "Pe"], ["pf2"])
         tt(T.xf[:], T.xd[:], T.Pe[:, 96:192], OP.mult, ["xd", "Pe"], ["xf"])
-        tt(T.Pf[:, 0:BLK], land[:, 3 * BLK:4 * BLK], T.Pe[:, 0:BLK], OP.max, [lk, "Pe"], ["Pf"])
+        tt(EX, EX, T.Pf[:, 96:192], OP.min, ["U5", "Pf"], ["U5"])
+        tt(SI, SI, T.Pf[:, 0:96], OP.min, ["U0", "Pf", "pf1", "pf2"], ["U0"])
         scan(T.xg[:], T.keep[:, 0:96], T.xf[:], OP.mult, OP.add, ["keep", "xf"], ["xg"])
-        tt(T.Pf[:, BLK:DS], land[:, 2 * BLK:3 * BLK], T.Pe[:, BLK:DS], OP.max, [lk, "Pe", "Pf"], ["pf2"])
         tt(T.s2[:, 0:6], gl, T.dsl[:, 0:6], OP.mult, ["xg", "dsl"], ["s2"])
-        tt(EX, EX, T.xe[:], OP.min, ["U5", "xe"], ["U5"])
-        tt(T.slf[:, 10:16], T.slf[:, 10:16], T.s2[:, 0:6], OP.add, ["slf", "s2"], ["slf"])
-        tt(SI, SI, T.Pf[:, 0:96], OP.min, ["U0", "Pf", "pf2"], ["U0"])
-        cp(T.sl16[:], T.slf[:], ["slf"], ["sl16"])
         tt(T.s1[:, 0:6], gl, T.edf[:, 0:6], OP.mult, ["xg", "edf"], ["s1"])
+        tt(T.slf[:, 10:16], T.slf[:, 10:16], T.s2[:, 0:6], OP.add, ["slf", "s2"], ["slf"])
+        tt(T.ST[:, 26:32], T.ST[:, 26:32], T.s1[:, 0:6], OP.add, ["cur", "s1"], ["cur"])
+        cp(T.sl16[:, 10:16], T.slf[:, 10:16], ["slf"], ["slg"])
+        ts(T.co[:, 10:16], T.ST[:, 26:32], 1.0 / X, OP.mult, ["cur"], ["co"])
 
     def start_guests():
-        tt(T.ST[:, 26:32], T.ST[:, 26:32], T.s1[:, 0:6], OP.add, ["cur", "s1"], ["cur"])
-        cp(T.co[:, 10:16], T.ST[:, 26:32], ["cur"], ["co"])
         gather_args(10, 16, ["A1"])
         fold_args(OWN, LANES, ["A1"])
 
     gather_args(0, 10, ["A0", "A1"])
-    mm(T.Ps[:, 0:OWN], T.W0[:], T.A[:, 0:OWN], False, True, ["W0r", "A0", "A1"], ["Ps"])
+    spread_arg0()
     fold_args(0, 160, ["A0", "A1"])
-    scan(T.hold[:, 0:OWN], T.head[:, 0:OWN], T.Ps[:, 0:OWN], OP.add, OP.min, ["head", "Ps"], ["hold"])
-    ts(T.sl16[:, 0:10], T.hold[:, 15:OWN:16], float(HALF), OP.add, ["hold"], ["sl16"])
+    hold_arg0()
+    held_list()
     fill0, fill1, fill2 = [], [], []
     for t in range(1, 9):
         nl = 160 if t <= 2 else 256
@@ -407,15 +429,30 @@ def build(core, T, topo):
         if t == 8:
             break
         st = stack_ops(min(t, 8 - t))
+        st[0]()
+        st[1]()
         if t % 2 == 1:
             gather_args(0, nl // 16, ["A0", "A1"])
             scatter(nl)
-            list_arg0(T.A, nl, ["A0", "A1"])
+            if t == 1:
+                spread_arg0()
+            else:
+                list_arg0(T.A, nl, ["A0", "A1"])
             fold_args(0, nl, ["A0", "A1"])
-            ts(T.sl16[:, 0:nl // 16], T.Ps[:, 0:nl // 16], float(HALF), OP.add, ["Ps"], ["sl16"])
-            fill0, fill1, fill2 = [], st[:6], st[6:]
+            if t == 1:
+                hold_arg0()
+            for f in st[2:4]:
+                f()
+            if t == 1:
+                held_list()
+            else:
+                ts(T.sl16[:, 0:nl // 16], T.Ps[:, 0:nl // 16], float(HALF), OP.add, ["Ps"], SL)
+            for f in st[4:-2][0:2]:
+                f()
+            fill0, fill1, fill2 = [], st[4:-2][2:] + st[-2:-1], st[-1:]
             if t == 7:
-                fill1, fill2 = [hole_flags, scatter_out], st
+                hole_flags()
+                fill1 = [st[-2], scatter_out]
         else:
             x = t // 2 - 1
             scatter(nl)
@@ -423,7 +460,7 @@ def build(core, T, topo):
             gather_args(0, 16, ["A0", "A1"])
             list_arg0(T.A, 256, ["A0", "A1"])
             fold_args(0, OWN, ["A0"])
-            for f in st:
+            for f in st[2:]:
                 f()
             if x == 0:
                 exchange_constants()
@@ -431,6 +468,7 @@ def build(core, T, topo):
                 for k, (a, b) in enumerate(MID):
                     ts(T.OUT[:, a:b], U[:, a:b], 16.0, OP.is_ge, ["Um"], ["O%d" % k], -33.0, OP.mult)
             ts(T.slf[:], T.Ps[:, 0:16], float(HALF), OP.add, ["Ps"], ["slf"])
+            ts(T.sl16[:, 0:10], T.Ps[:, 0:10], float(HALF), OP.add, ["Ps"], ["slo"])
             if x == 0:
                 ts(T.AE[:], AG[:, 0:WT].indirect(T.ec16[:, 0:6]), float(HALF), OP.subtract, ["AG", "AGr", "ec16"], ["AE"])
                 list_arg0(T.AE, 96, ["AE"])
@@ -447,15 +485,14 @@ def build(core, T, topo):
             if x == 2:
                 for k, (a, b) in enumerate(MID):
                     dma("g", T.OUT[:, a:b], U[:, a:b], ["Um", "L2", "O%d" % k], ["O%d" % k], True)
-                fill2 = [unfold_ends]
 
+    mm(T.Pe[:, 0:16], T.Wr[:], T.NX[:, 1:32:2], True, True, ["Wr", "NX"], ["Pe"])
     scatter_out()
     dma("y", T.yv[:, 0:HALF], T.OUT[:, 0:HALF], OK, ["yv0"])
     dma("s", T.yv[:, HALF:W], T.OUT[:, HALF:W], OK, ["yv1"])
-    mm(T.Pe[:, 0:16], T.Wr[:], T.NX[:, 0:16], True, True, ["Wr", "NX"], ["Pe"])
-    ts(T.s1[:], T.Pe[:, 0:16], float(W), OP.is_ge, ["Pe"], ["s1"], -8192.0, OP.mult)
+    ts(T.s1[:], T.Pe[:, 0:16], W * X, OP.is_ge, ["Pe"], ["s1"], -8192.0 * X, OP.mult)
     tt(T.s2[:], T.s1[:], T.Pe[:, 0:16], OP.add, ["s1", "Pe"], ["s2"])
-    ts(T.yo[:], T.s2[:], -1.0, OP.max, ["s2"], ["yo"])
+    ts(T.yo[:], T.s2[:], 1.0 / X, OP.mult, ["s2"], ["yo"], -1.0, OP.max)
     dma("y", T.ya[:], T.yo[:], ["yo"], ["ya"])
     return ops
 

from concourse.bass import DstId, RemoteDMATransfer
from concourse.mybir import AluOpType, ActivationFunctionType

OP = AluOpType
AF = ActivationFunctionType
W, OWN, BLK, DS, LANES, NR = 3072, 160, 48, 96, 256, 4
WT = W + LANES
HOLE, THUNK = 31.0, 32.0
HALF = 1536
TOL = 3.0 * 2.0 ** -13
BIG = 2.0 ** 27
X = 16.0
KV = {160: 4, 256: 9}
NE = 720
SPLIT = {160: (34, 30, 16), 256: (56, 48, 24)}

F32, BF, F16, I32, U16 = "float32", "bfloat16", "float16", "int32", "uint16"


def _sb(n, d):
    return ("sbuf", [128, n], d)


SCRATCH = {
    "AG": _sb(WT, I32), "VR": _sb(W, BF), "U": _sb(WT, BF), "OUT": _sb(WT, BF),
    "rti": _sb(16, I32), "rtf": _sb(16, F32),
    "pi": _sb(8, I32), "pc": _sb(32, F32), "io_c": _sb(144, BF), "io_s": _sb(256, BF), "io_g": _sb(128, BF),
    "io_h": _sb(128, BF), "io_t": _sb(896, BF), "io_k": _sb(96, F32),
    "Wsl": _sb(144, F16), "Wd": _sb(144, F16), "Wf": _sb(144, F16), "Wy": _sb(128, F16), "W0": _sb(128, F16), "Wz": _sb(128, BF),
    "Wlo": _sb(128, BF), "Whi": _sb(128, BF), "Wc": _sb(128, BF), "Wc4": _sb(128, BF), "Ip": _sb(128, BF), "In": _sb(128, BF),
    "Wr": _sb(128, F32), "ones": _sb(256, BF), "lad": _sb(896, BF), "nm": _sb(256, BF), "keep": _sb(256, BF),
    "head": _sb(256, BF), "md": _sb(256, BF), "am": _sb(96, BF), "mE": _sb(NE, BF), "zo": _sb(4, U16), "hol": _sb(160, BF),
    "ecf": _sb(16, F32), "ec16": _sb(16, U16), "edf": _sb(16, F32), "slE": _sb(16, F32), "slf": _sb(16, F32), "dsl": _sb(16, F32),
    "A": _sb(256, F16), "AE": _sb(96, F16), "sl16": _sb(16, U16), "ind": _sb(256, BF), "sv": _sb(256, BF),
    "tm": _sb(128, F32), "t2": _sb(128, F32), "O16": _sb(128, U16), "V": _sb(2048, BF), "SO": _sb(2048, BF),
    "m": _sb(256, BF), "y": _sb(256, F16), "tb": _sb(256, BF), "ab": _sb(256, BF), "dat": _sb(256, BF), "tn": _sb(256, BF),
    "hold": _sb(256, F32), "eq": _sb(256, BF),
    "SD": _sb(256, BF), "E": _sb(NE, BF), "Z": _sb(NE + 16, BF), "junk": _sb(4096, BF), "acc": _sb(16, F32),
    "ST": _sb(112, F32), "DL": _sb(112, F32), "dn": _sb(16, F32), "s1": _sb(16, F32), "s2": _sb(16, F32),
    "s3": _sb(16, F32), "s4": _sb(16, F32), "s5": _sb(16, F32), "s6": _sb(16, F32), "ri": _sb(16, I32),
    "XB": _sb(64, F32), "DB": _sb(64, F32), "NX": _sb(64, F32),
    "co": _sb(32, U16), "ent": _sb(16, F32), "pa": _sb(64, F32), "pb": _sb(64, F32),
    "L0": _sb(192, BF), "L1": _sb(192, BF), "L2": _sb(192, BF), "stg": _sb(96, BF),
    "xc": _sb(96, BF), "xd": _sb(96, BF), "xf": _sb(96, BF), "xg": _sb(96, BF),
    "yo": _sb(16, F32),
    "Pq": ("psum", [128, 512], F32), "Pr": ("psum", [128, 512], F32), "Pc": ("psum", [128, 512], F32),
    "Po": ("psum", [128, 512], F32), "Ps": ("psum", [128, 512], F32), "Pd": ("psum", [128, 512], F32),
    "Pe": ("psum", [128, 512], F32), "Pf": ("psum", [128, 512], F32),
}
SEMAPHORES = (["qv", "qs", "qt", "qg"] + [n + str(x) for n in ("near", "far", "arr") for x in range(3)]
              + ["d%d" % i for i in range(12)])


def build(core, T, topo):
    ops = []
    rank = T.rank_of(core)

    def add(q, fn, r, w, kind="c"):
        ops.append((q, fn, list(r), list(w), kind))

    def ts(out, in0, s1, o0, r, w, s2=None, o1=None):
        if o1 is None:
            add("v", lambda e: e.tensor_scalar(out, in0, s1, None, o0), r, w)
        else:
            add("v", lambda e: e.tensor_scalar(out, in0, s1, s2, o0, o1), r, w)

    def tt(out, a, b, o, r, w):
        add("v", lambda e: e.tensor_tensor(out, a, b, o), r, w)

    def cp(out, a, r, w):
        add("v", lambda e: e.tensor_copy(out, a), r, w)

    def ms(out, c, w):
        add("v", lambda e: e.memset(out, c), [], w)

    def scan(out, d0, d1, o0, o1, r, w):
        add("v", lambda e: e.tensor_tensor_scan(out, d0, d1, 0.0, o0, o1), r, w)

    def act(out, a, f, r, w, bias=0.0, scale=1.0, acc=None):
        add("s", lambda e: e.activation(out, a, f, bias=bias, scale=scale, accum_out=acc), r, w)

    def mm(out, l, rh, st, sp, r, w):
        add("t", lambda e: e.matmul(out, l, rh, st, sp), r, w)

    def iota(out, pat, base, cm, w, flt=True):
        if flt:
            add("g", lambda e: e.iota(out, pat, base, cm, allow_small_or_imprecise_dtypes=True), [], w)
        else:
            add("g", lambda e: e.iota(out, pat, base, cm), [], w)

    def dma(q, out, a, r, w, accum=False):
        if accum:
            add(q, lambda e: e.dma_start(out, a, accum_op=OP.add), r, w, "d")
        else:
            add(q, lambda e: e.dma_start(out, a), r, w, "d")

    U, AG, pc = T.U, T.AG, T.pc
    Uw = U[:, 0:WT]
    UK = ["U0", "U1", "U2", "U3", "U4", "U5", "Ur", "Um"]
    OK = ["O0", "O1", "O2", "O3", "Or"]
    SL = ["slo", "slg"]
    MID = ((DS, HALF), (HALF, W - DS))
    QB = ((T.Pf, "Pf"), (T.Pq, "Pq"), (T.Pr, "Pr"))

    def col(j):
        return pc[:, j:j + 1]

    dma("s", T.rti[:, 0:10], T.rts[:], [], ["rti"])
    dma("y", T.VR[:, 0:HALF], T.vals[:, 0:HALF], [], ["VR0"])
    dma("y", T.VR[:, HALF:W], T.vals[:, HALF:W], [], ["VR1"])
    dma("y", AG[:, 0:W], T.ag[:], [], ["AG"])

    def aff(j, src, rk, scale, bias):
        act(col(j), src, AF.Identity, rk, ["c%d" % j], bias=bias, scale=scale)

    iota(T.pi[:, 0:1], [[0, 1]], 0, 1, ["pi0"], False)
    iota(T.io_c[:], [[1, 144]], 0, 0, ["io_c"])
    iota(T.io_k[:], [[0, 6], [256, 16]], 0, 0, ["io_k"])
    iota(T.io_h[:], [[1, 16], [0, 8]], 0, 0, ["io_h"])
    iota(T.io_g[:], [[1, 8], [0, 16]], 0, 0, ["io_g"])
    iota(T.io_s[:], [[0, 16], [1, 16]], 0, 0, ["io_s"])
    iota(AG[:, W:WT], [[0, LANES]], W, 0, ["AGr"], False)
    iota(T.io_t[:], [[0, 112], [1, 8]], 0, 0, ["io_t"])
    ms(U[:, W:WT], HOLE, ["Ur"])
    ms(T.hol[:], HOLE, ["hol"])
    ms(T.ones[:], 1.0, ["ones"])
    ts(T.pi[:, 1:2], T.pi[:, 0:1], 15, OP.bitwise_and, ["pi0"], ["pi1"])
    ts(T.pi[:, 2:3], T.pi[:, 0:1], 4, OP.logical_shift_right, ["pi0"], ["pi2"])
    ts(T.pi[:, 3:4], T.pi[:, 0:1], 7, OP.bitwise_and, ["pi0"], ["pi3"])
    ms(T.acc[:], 0.0, ["acc"])
    cp(pc[:, 0:4], T.pi[:, 0:4], ["pi0", "pi1", "pi2", "pi3"], ["c0"])
    P, I, G, TT = col(0), col(1), col(2), col(3)
    c0 = ["c0"]
    ms(T.Z[:, 0:16], -TOL, ["Zc"])
    ms(T.Z[:, 16:NE + 16], 0.0, ["Z"])
    ts(col(6), I, 0.0, OP.is_equal, c0, ["c6"])
    ts(col(9), I, 8.0, OP.is_ge, c0, ["c9"])
    ts(col(13), I, 1.0, OP.is_equal, c0, ["c13"], 8192.0 * X, OP.mult)
    ts(col(28), P, 2.0, OP.is_equal, c0, ["c28"], 4.0, OP.mult)
    aff(7, P, c0, 1.0, 15.0)
    aff(4, G, c0, 16.0, 15.0)
    aff(29, I, c0, X, W * X)
    aff(11, G, c0, 2.0, 0.0)
    aff(12, G, c0, 2.0, 1.0)
    aff(5, I, ["c0", "c7"], -2.0, col(7))
    aff(8, TT, ["c0", "c4"], -1.0, col(4))
    aff(10, col(9), ["c9"], -2.0, 1.0)
    aff(14, col(6), ["c6", "c13"], -131072.0 * X, col(13))
    aff(15, col(13), ["c13"], 192.0 / 8192.0, 0.0)
    aff(18, col(6), ["c6"], -1.875, 2.0)
    aff(19, col(6), ["c6"], 15.0, 16.0)
    aff(20, TT, c0, 2.0, 18.0)
    aff(25, I, c0, 8.0, 8.0)
    aff(17, col(6), ["c6", "c15"], 491520.0 * X, col(15))
    aff(21, col(6), ["c6", "c20"], 13.125, col(20))
    aff(26, col(25), ["c25", "c0"], I, 0.0)
    aff(30, col(28), ["c28", "c17"], 1.0, col(17))
    aff(22, col(9), ["c9", "c21"], -100.0, col(21))
    aff(16, col(21), ["c21"], 1.0, -100.0)
    aff(24, I, c0, -1.0, 15.0)
    aff(23, col(9), ["c9", "c16"], 100.0, col(16))
    act(T.keep[:], T.io_s[:], AF.Tanh, ["io_s"], ["keep"], scale=20.0)
    ms(T.SD[:], 0.0, ["SD"])
    ms(T.DB[:], 0.0, ["DB0", "Dq", "De"])
    ms(T.hold[:, OWN:LANES], 1.0e5 * X, ["hold"])
    ms(T.mE[:], 2.0, ["mE"])
    ts(T.Wr[:], T.io_c[:, 0:128], col(5), OP.is_equal, ["io_c", "c5"], ["Wr"])
    ts(T.ST[:, 16:112], T.io_k[:], col(29), OP.add, ["io_k", "c29"], ["cur", "S"])
    ms(T.mE[:, 0:17:16], -1.0, ["mE"])
    ts(T.Wsl[:], T.io_c[:], col(7), OP.is_equal, ["io_c", "c6", "c7"], ["Wsl"], col(6), OP.mult)
    ts(T.Ip[:], T.io_c[:, 0:128], P, OP.is_equal, ["io_c", "c0"], ["Ip"])
    ms(T.mE[:, 48:97:48], -1.0, ["mE"])
    ts(T.In[:], T.io_c[:, 0:128], P, OP.is_equal, ["io_c", "c0"], ["In"], -1.0, OP.mult)
    ts(T.rtf[:, 0:10], T.rti[:, 0:10], X, OP.mult, ["rti"], ["rtf"])
    mm(T.Pe[:, 0:10], T.Wr[:], T.rtf[:, 0:10], True, True, ["Wr", "rtf"], ["Pe"])
    ts(T.Wd[:], T.io_c[:], col(8), OP.is_equal, ["io_c", "c8", "c10"], ["Wd"], col(10), OP.mult)
    ts(T.Wf[:], T.io_c[:], col(8), OP.is_equal, ["io_c", "c8", "c9"], ["Wf"], col(9), OP.mult)
    ts(T.Wlo[:], T.io_h[:], col(11), OP.is_equal, ["io_h", "c11"], ["Wlo"])
    ts(T.Whi[:], T.io_h[:], col(12), OP.is_equal, ["io_h", "c12"], ["Whi"])
    ts(T.Wy[:], T.io_g[:], G, OP.is_equal, ["io_g", "c0"], ["Wy"], X, OP.mult)
    ts(T.Wz[:], T.io_g[:], G, OP.is_equal, ["io_g", "c0", "c14"], ["Wz"], col(14), OP.mult)
    cp(T.ST[:, 16:26], T.Pe[:, 0:10], ["Pe"], ["cur"])
    ts(T.Wc[:], T.ones[:, 0:128], col(17), OP.mult, ["ones", "c17"], ["Wc"])
    ts(T.co[:, 0:16], T.ST[:, 16:32], 1.0 / X, OP.mult, ["cur"], ["co"])
    ts(T.Wc4[:], T.ones[:, 0:128], col(30), OP.mult, ["ones", "c30"], ["Wc4"])
    ts(T.nm[:], T.io_s[:], I, OP.not_equal, ["io_s", "c0"], ["nm"], BIG, OP.mult)
    ts(T.md[:], T.io_s[:], I, OP.is_gt, ["io_s", "c0"], ["md"])
    ts(T.W0[:], T.io_g[:], G, OP.is_equal, ["io_g", "c0", "c6"], ["W0r"], col(6), OP.mult)

    def ends(n, nl):
        ts(col(27), I, KV[nl] + 0.5, OP.is_lt, ["c0", "c26"], ["c27"], col(26), OP.mult)
        ts(T.zo[:, 2 * n:2 * n + 1], col(27), 15.0, OP.add, ["c27"], ["zo%d" % n])

    ends(0, 160)
    banks = ((T.Pq, "Pq"), (T.Pr, "Pr"), (T.Pc, "Pc"), (T.Po, "Po"), (T.Pd, "Pd"), (T.Pf, "Pf"))
    for k, (pb, pk) in enumerate(banks):
        act(pb[:], T.VR[:, 512 * k:512 * k + 512], AF.Relu, ["VR%d" % (k // 3)], [pk], scale=-THUNK)
    for k, (pb, pk) in enumerate(banks):
        tt(U[:, 512 * k:512 * k + 512], T.VR[:, 512 * k:512 * k + 512], pb[:], OP.max, ["VR%d" % (k // 3), pk], ["U%d" % k])
    act(T.lad[:], T.io_t[:], AF.Identity, ["io_t", "c18", "c19"], ["lad"], bias=col(19), scale=col(18))
    act(T.head[:], T.keep[:], AF.Identity, ["keep"], ["head"], bias=2.0 * BIG, scale=-2.0 * BIG)
    cp(Uw.indirect(T.co[:, 0:10]), T.hol[:], ["co", "hol"] + UK, UK)
    ms(T.lad[:, 0::8], 0.0, ["lad"])

    def exchange_constants():
        ts(T.ecf[:, 0:6], T.io_k[:, 0:6], col(29), OP.subtract, ["io_k", "c29"], ["ecf"], (2 * W - DS + 15) * X, OP.add)
        ts(T.am[:], T.io_s[:, 0:96], col(24), OP.is_equal, ["io_s", "c24"], ["am"])
        ts(T.ec16[:, 0:6], T.ecf[:, 0:6], 1.0 / X, OP.mult, ["ecf"], ["ec16"])
        tt(T.edf[:, 0:6], T.ecf[:, 0:6], T.ST[:, 106:112], OP.subtract, ["ecf", "S"], ["edf"])
        ends(1, 256)
        for k in range(5, KV[256] + 1):
            ms(T.mE[:, 8 * k * (k - 1):8 * k * (k - 1) + 1], -1.0, ["mE"])

    def gather_args(k0, k1, key):
        ts(T.A[:, 16 * k0:16 * k1], AG[:, 0:WT].indirect(T.co[:, k0:k1]), float(HALF), OP.subtract,
           ["AG", "AGr", "co"], key)

    def list_arg0(src, nl, key):
        for r in range(16):
            mm(T.Ps[:, 0:nl // 16], T.Wsl[:, 15 - r:143 - r], src[:, r:nl:16], r == 0, r == 15, ["Wsl"] + key, ["Ps"])

    def spread_arg0():
        mm(T.Ps[:, 0:OWN], T.Ip[:], T.nm[:, 0:OWN], True, False, ["Ip", "nm"], ["Ps"])
        mm(T.Ps[:, 0:OWN], T.W0[:], T.A[:, 0:OWN], False, True, ["W0r", "A0", "A1"], ["Ps"])

    def hold_arg0():
        scan(T.hold[:, 0:OWN], T.head[:, 0:OWN], T.Ps[:, 0:OWN], OP.add, OP.min, ["head", "Ps"], ["hold"])

    def held_list():
        ts(T.sl16[:, 0:10], T.hold[:, 15:OWN:16], float(HALF), OP.add, ["hold"], SL)

    def fold_args(l0, l1, key):
        for n, wt, wk in ((0, T.Wd, "Wd"), (128, T.Wf, "Wf")):
            for h in range(2):
                mm(T.Po[:, n + l0 // 2:n + l1 // 2], wt[:, 8 - 8 * h:136 - 8 * h], T.A[:, l0 + h:l1:2], h == 0, h == 1,
                   [wk] + key, ["Po"])

    def deltas(depth):
        n = 16 * (depth + 1)
        tt(T.DL[:, 32:32 + n], T.ST[:, 16:16 + n], T.ST[:, 32:32 + n], OP.subtract, ["cur", "S"], ["DL"])

    def stack_ops(depth):
        o = [lambda: tt(T.ent[:], T.NX[:, 1:32:2], T.XB[:, 1:32:2], OP.not_equal, ["NX", "q"], ["ent"]),
             lambda: cp(T.ST[:, 16:32], T.NX[:, 1:32:2], ["NX"], ["cur"])]
        for d in range(1, depth + 1):
            o.append(lambda d=d: tt(T.pb[:, 16 * d - 16:16 * d], T.dn[:], T.DL[:, 16 * d + 32:16 * d + 48], OP.mult,
                                    ["dn", "DL"], ["pb%d" % d]))
            o.append(lambda d=d: tt(T.pa[:, 16 * d - 16:16 * d], T.ent[:], T.DL[:, 16 * d + 16:16 * d + 32], OP.mult,
                                    ["ent", "DL"], ["pa%d" % d]))
        n = 16 * depth
        o.append(lambda: tt(T.ST[:, 32:32 + n], T.ST[:, 32:32 + n], T.pb[:, 0:n], OP.subtract,
                            ["S"] + ["pb%d" % d for d in range(1, depth + 1)], ["S"]))
        o.append(lambda: tt(T.ST[:, 32:32 + n], T.ST[:, 32:32 + n], T.pa[:, 0:n], OP.add,
                            ["S"] + ["pa%d" % d for d in range(1, depth + 1)], ["S"]))
        return o

    def unfold_ends():
        for k, a, uk, tmp, tk in ((2, 0, "U0", T.xc, "xc"), (3, W - DS, "U5", T.xd, "xd")):
            ts(tmp[:], U[:, a:a + DS], 16.0, OP.is_ge, [uk], [tk], -33.0, OP.mult)
        for k, a, uk, tmp, tk in ((2, 0, "U0", T.xc, "xc"), (3, W - DS, "U5", T.xd, "xd")):
            tt(T.OUT[:, a:a + DS], U[:, a:a + DS], tmp[:], OP.add, [uk, tk], ["O%d" % k])

    def hole_flags():
        ts(T.tn[:], T.SO[:, 7:2048:8], 16.0, OP.is_ge, ["R0", "R1", "R2"], ["tn"], -33.0, OP.mult)

    def scatter_out():
        tt(T.OUT[:, 0:WT].indirect(T.co[:, 16:32]), T.dat[:], T.tn[:], OP.add, ["co", "dat", "tn"] + OK, OK)

    def step(t, nl, fill0, fill1, fill2):
        M, KC, kv = nl // 2, nl // 16, KV[nl]
        depth = min(t, 8 - t)
        kh = (KC + 2) // 4 * 2
        (v0, v1, vk), (s0, s1, sk) = ((10, 16, ["slg"]), (0, 10, ["slo"])) if fill0 else ((0, kh, SL), (kh, KC, SL))
        act(T.ind[:, 16 * s0:16 * s1], Uw.indirect(T.sl16[:, s0:s1]), AF.Sign, UK + sk, ["ind1"], bias=-7.5)
        ts(T.ind[:, 16 * v0:16 * v1], Uw.indirect(T.sl16[:, v0:v1]), 8.0, OP.is_ge, UK + vk, ["ind0"], 0.5, OP.subtract)
        act(T.sv[:, 0:nl], Uw.indirect(T.sl16[:, 0:KC]), AF.Copy, UK + SL, ["sv"])
        mm(T.Pc[:, 0:M], T.Wlo[:], T.ind[:, 0:nl:2], True, False, ["Wlo", "ind0", "ind1"], ["Pc"])
        mm(T.Pc[:, 0:M], T.Whi[:], T.ind[:, 1:nl:2], False, True, ["Whi", "ind0", "ind1"], ["Pc"])
        for f in fill0:
            f()
        for pq, pk in QB:
            mm(pq[:, 0:nl], T.Wc4[:] if pk == "Pr" else T.Wc[:], T.ones[:, 0:nl], True, False, ["Wc", "Wc4", "ones"], [pk])
        mm(T.Pf[:, 0:nl], T.Ip[:], T.nm[:, 0:nl], False, False, ["Ip", "nm"], ["Pf"])
        mm(T.Pd[:, 0:nl], T.In[:], T.sv[:, 0:nl], True, False, ["In", "sv"], ["Pd"])
        for f in fill1:
            f()
        a, b, c = SPLIT[nl]
        hv = ((0, 0, a), (1, a, M))
        for n, lo, hi in hv:
            ts(T.tm[:, lo:hi], T.Pc[:, lo:hi], 0.5, OP.is_ge, ["Pc"], ["tm%d" % n])
        for n, lo, hi in hv:
            tt(T.t2[:, lo:hi], T.tm[:, lo:hi], T.Po[:, lo:hi], OP.mult, ["tm%d" % n, "Po"], ["t2%d" % n])
        for n, lo, hi in hv:
            tt(T.Pe[:, 256 + lo:256 + hi], T.t2[:, lo:hi], T.Po[:, 128 + lo:128 + hi], OP.add, ["t2%d" % n, "Po"], ["oc%d" % n])
        for n, lo, hi in hv:
            ts(T.O16[:, lo:hi], T.Pe[:, 256 + lo:256 + hi], float(HALF), OP.add, ["oc%d" % n], ["of%d" % n])
        parts = ((0, a), (a, a + b), (a + b, M))
        for n in (0, 2):
            lo, hi = parts[n]
            act(T.V[:, 16 * lo:16 * hi], Uw.indirect(T.O16[:, lo:hi]), AF.Copy, UK + ["of%d" % (n // 2)], ["V%d" % n])
        lo, hi = parts[1]
        cp(T.XB[:, 33:64:2], T.ST[:, 16:32], ["cur"], ["xc1"])
        cp(T.V[:, 16 * lo:16 * hi], Uw.indirect(T.O16[:, lo:hi]), UK + ["of1"], ["V1"])
        for n in (1, 0, 2):
            lo, hi = parts[n]
            scan(T.SO[:, 16 * lo:16 * hi], T.lad[:, 0:16 * (hi - lo)], T.V[:, 16 * lo:16 * hi], OP.min, OP.max,
                 ["lad", "V%d" % n], ["R%d" % n])
            for pq, pk in QB:
                mm(pq[:, 2 * lo:2 * hi], T.Wz[:], T.SO[:, 16 * lo + 7:16 * hi:8], False, False, ["Wz", "R%d" % n], [pk])
        RK = ["R0", "R1", "R2"]
        R = T.SO[:, 7:8 * nl:8]
        mm(T.Pd[:, 0:nl], T.Ip[:], R, False, False, ["Ip"] + RK, ["Pd"])
        act(T.tb[:, 0:nl], R, AF.Relu, RK, ["tb"], bias=-1920.0, scale=128.0)
        for f in fill2:
            f()
        ts(T.m[:, 0:M], T.SO[:, 7:8 * nl:16], col(22), OP.is_equal, RK + ["c22"], ["m0"])
        ts(T.m[:, 128:128 + M], T.SO[:, 15:8 * nl:16], col(23), OP.is_equal, RK + ["c23"], ["m1"])
        yv = ((0, 0, M // 2), (1, M // 2, M)) if nl == LANES else ((1, 0, M),)
        for n, lo, hi in yv:
            for h in range(2):
                tt(T.y[:, 2 * lo + h:2 * hi:2], T.m[:, 128 * h + lo:128 * h + hi], T.Pe[:, 256 + lo:256 + hi], OP.mult,
                   ["m%d" % h, "oc0", "oc1"], ["y%d%d" % (n, h)])
            mm(T.Pf[:, 2 * lo:2 * hi], T.Wy[:], T.y[:, 2 * lo:2 * hi], False, n == 1, ["Wy", "y%d0" % n, "y%d1" % n], ["Pf"])
        for pq, pk in QB[1:]:
            mm(pq[:, 0:nl], T.Wy[:], T.y[:, 0:nl], False, True, ["Wy", "y00", "y01", "y10", "y11"], [pk])
        mm(T.Pd[:, 0:nl], T.Ip[:], T.tb[:, 0:nl], False, True, ["Ip", "tb"], ["Pd"])
        if t == 7:
            unfold_ends()
        if t == 8:
            hole_flags()
        scan(T.hold[:, 0:nl], T.head[:, 0:nl], T.Pf[:, 0:nl], OP.add, OP.min, ["head", "Pf"], ["hold"])
        deltas(depth)
        for k in range(KC - 1, kv, -1):
            act(T.junk[:, 256 * k:256 * k + 16 * k], T.Pr[:, 0:16 * k], AF.Tanh, ["Pr", "hold"], ["acc%d" % k],
                bias=T.hold[:, 16 * k + 15:16 * k + 16], scale=-1.0, acc=T.acc[:, k:k + 1])
        act(T.ab[:, 0:nl], T.Pd[:, 0:nl], AF.Relu, ["Pd"], ["ab"], bias=HOLE, scale=-1.0)
        act(T.dat[:, 0:nl], T.ab[:, 0:nl], AF.Relu, ["ab"], ["dat"], bias=HOLE, scale=-1.0)
        q = T.hold[:, 15:256:16]
        tt(T.eq[:, 0:nl], T.hold[:, 0:nl], T.Pq[:, 0:nl], OP.is_equal, ["hold", "Pq"], ["eq"])
        for k in range(1, kv + 1):
            o = 8 * k * (k - 1)
            ts(T.E[:, o:o + 16 * k], T.Pq[:, 0:16 * k], T.hold[:, 16 * k + 15:16 * k + 16], OP.is_equal,
               ["Pq", "hold"], ["E%d" % k], -TOL, OP.add)
            if k == 2:
                scan(T.SD[:, 0:nl], T.eq[:, 0:nl], T.md[:, 0:nl], OP.max, OP.min, ["eq", "md"], ["SD"])
        ts(T.s1[:], q, W * X, OP.is_ge, ["hold"], ["s1"])
        ts(T.dn[:], q, 1.0e6 * X, OP.is_ge, ["hold"], ["dn"])
        ne = 8 * kv * (kv + 1)
        scan(T.Z[:, 16:16 + ne], T.mE[:, 0:ne], T.E[:, 0:ne], OP.min, OP.max,
             ["mE"] + ["E%d" % k for k in range(1, kv + 1)], ["Z"])
        tt(T.s3[:], T.s1[:], T.SD[:, 15:256:16], OP.add, ["s1", "SD"], ["s3"])
        tt(T.DB[:, 33:64:2], q, T.ST[:, 16:32], OP.subtract, ["hold", "cur"], ["Dq"])
        ts(T.s2[:], q, DS * X, OP.is_ge, ["hold"], ["s2"])
        zc = 0 if nl == 160 else 2
        AK = ["acc"] + ["acc%d" % k for k in range(kv + 1, KC)]
        tt(T.s5[:], T.Z[:, 0:NE + 16].indirect(T.zo[:, zc:zc + 1]), T.s3[:], OP.add, ["Z", "Zc", "zo%d" % (zc // 2), "s3"], ["s5"])
        tt(T.s4[:], T.dn[:], T.DL[:, 32:48], OP.mult, ["dn", "DL"], ["s4"])
        cp(T.ri[:], T.acc[:], AK, ["ri"])
        tt(T.s6[:], T.s5[:], T.acc[:], OP.add, ["s5"] + AK, ["s6"])
        tt(T.DB[:, 1:32:2], T.DB[:, 33:64:2], T.s2[:], OP.mult, ["Dq", "s2"], ["De"])
        tt(T.XB[:, 1:32:2], T.ST[:, 16:32], T.s4[:], OP.subtract, ["cur", "s4"], ["q"])
        tt(T.XB[:, 0:32:2], T.s6[:], T.ri[:], OP.is_le, ["s6", "ri"], ["W0"])
        tt(T.XB[:, 32:64:2], T.s6[:], T.ri[:], OP.is_le, ["s6", "ri"], ["W1"])
        scan(T.NX[:], T.DB[:], T.XB[:], OP.mult, OP.add, ["DB0", "Dq", "De", "q", "xc1", "W0", "W1"], ["NX"])
        ts(T.co[:], T.NX[:, 1:64:2], 1.0 / X, OP.mult, ["NX"], ["co"])

    def scatter(nl):
        cp(Uw.indirect(T.co[:, 16:16 + nl // 16]), T.dat[:, 0:nl], ["co", "dat"] + UK, UK)

    def bits(engines):
        mask = 0
        for e in engines:
            mask |= 1 << e
        return mask

    def exchange(x):
        land, arr = T["L%d" % x], T.sem["arr%d" % x]
        up, down, far = (T.cores[(rank + d) % NR] for d in (1, NR - 1, 2))
        both = [e for e in topo.engines(core, up) if e in topo.engines(core, down)]
        per = len(both) // 2
        trs = []
        for n, (dst, src, out) in enumerate(((up, U[:, 0:BLK], land[:, 0:BLK]),
                                             (down, U[:, W - DS:W - BLK], land[:, 3 * BLK:4 * BLK]))):
            ad = topo.addr(dst)
            trs.append(RemoteDMATransfer(dst_ids=[DstId(rid=ad[0], pnc=ad[1])], dma_engine_mask=bits(both[n * per:(n + 1) * per]),
                                         remote_sem=arr, src=src, dst=out))
        add("g", lambda e: e.remote_dma_fused(trs, local_sem=T.sem["near%d" % x]), UK, [], ("near%d" % x, 2 * per))
        act(T.stg[:, 0:BLK], U[:, BLK:DS], AF.Copy, ["U0"], ["stg0"])
        act(T.stg[:, BLK:DS], U[:, W - BLK:W], AF.Copy, ["U5"], ["stg1"])
        ad, nf = topo.addr(far), len(topo.engines(core, far))
        add("g", lambda e: e.remote_dma(land[:, BLK:3 * BLK], T.stg[:], arr, T.sem["far%d" % x], ad[1], ad[0], topo.mask(core, far)),
            ["stg0", "stg1"], [], ("far%d" % x, nf))
        return 2 * per + nf

    def after_exchange(x, total):
        land = T["L%d" % x]
        lk = "L%d" % x
        add("x", None, [], [lk], ("arr%d" % x, total))
        EX, SI = U[:, W - DS:W], U[:, 0:DS]
        gl = T.xg[:, 15:96:16]
        ts(T.Pf[:, 96:192], land[:, 0:DS], HOLE, OP.not_equal, [lk], ["Pf"], HOLE, OP.add)
        ts(T.xd[:], land[:, 0:DS], HOLE, OP.is_equal, [lk], ["xd"])
        tt(T.Pf[:, 0:BLK], land[:, 3 * BLK:4 * BLK], T.Pe[:, 0:BLK], OP.max, [lk, "Pe"], ["pf1"])
        tt(T.Pf[:, BLK:DS], land[:, 2 * BLK:3 * BLK], T.Pe[:, BLK:DS], OP.max, [lk, "Pe"], ["pf2"])
        tt(T.xf[:], T.xd[:], T.Pe[:, 96:192], OP.mult, ["xd", "Pe"], ["xf"])
        tt(EX, EX, T.Pf[:, 96:192], OP.min, ["U5", "Pf"], ["U5"])
        tt(SI, SI, T.Pf[:, 0:96], OP.min, ["U0", "Pf", "pf1", "pf2"], ["U0"])
        scan(T.xg[:], T.keep[:, 0:96], T.xf[:], OP.mult, OP.add, ["keep", "xf"], ["xg"])
        tt(T.s2[:, 0:6], gl, T.dsl[:, 0:6], OP.mult, ["xg", "dsl"], ["s2"])
        tt(T.s1[:, 0:6], gl, T.edf[:, 0:6], OP.mult, ["xg", "edf"], ["s1"])
        tt(T.slf[:, 10:16], T.slf[:, 10:16], T.s2[:, 0:6], OP.add, ["slf", "s2"], ["slf"])
        tt(T.ST[:, 26:32], T.ST[:, 26:32], T.s1[:, 0:6], OP.add, ["cur", "s1"], ["cur"])
        cp(T.sl16[:, 10:16], T.slf[:, 10:16], ["slf"], ["slg"])
        ts(T.co[:, 10:16], T.ST[:, 26:32], 1.0 / X, OP.mult, ["cur"], ["co"])

    def start_guests():
        gather_args(10, 16, ["A1"])
        fold_args(OWN, LANES, ["A1"])

    gather_args(0, 10, ["A0", "A1"])
    spread_arg0()
    fold_args(0, 160, ["A0", "A1"])
    hold_arg0()
    held_list()
    fill0, fill1, fill2 = [], [], []
    for t in range(1, 9):
        nl = 160 if t <= 2 else 256
        step(t, nl, fill0, fill1, fill2)
        if t == 8:
            break
        st = stack_ops(min(t, 8 - t))
        st[0]()
        st[1]()
        if t % 2 == 1:
            gather_args(0, nl // 16, ["A0", "A1"])
            scatter(nl)
            if t == 1:
                spread_arg0()
            else:
                list_arg0(T.A, nl, ["A0", "A1"])
            fold_args(0, nl, ["A0", "A1"])
            if t == 1:
                hold_arg0()
            for f in st[2:4]:
                f()
            if t == 1:
                held_list()
            else:
                ts(T.sl16[:, 0:nl // 16], T.Ps[:, 0:nl // 16], float(HALF), OP.add, ["Ps"], SL)
            for f in st[4:-2][0:2]:
                f()
            fill0, fill1, fill2 = [], st[4:-2][2:] + st[-2:-1], st[-1:]
            if t == 7:
                hole_flags()
                fill1 = [st[-2], scatter_out]
        else:
            x = t // 2 - 1
            scatter(nl)
            total = exchange(x)
            gather_args(0, 16, ["A0", "A1"])
            list_arg0(T.A, 256, ["A0", "A1"])
            fold_args(0, OWN, ["A0"])
            for f in st[2:]:
                f()
            if x == 0:
                exchange_constants()
            if x == 2:
                for k, (a, b) in enumerate(MID):
                    ts(T.OUT[:, a:b], U[:, a:b], 16.0, OP.is_ge, ["Um"], ["O%d" % k], -33.0, OP.mult)
            ts(T.slf[:], T.Ps[:, 0:16], float(HALF), OP.add, ["Ps"], ["slf"])
            ts(T.sl16[:, 0:10], T.Ps[:, 0:10], float(HALF), OP.add, ["Ps"], ["slo"])
            if x == 0:
                ts(T.AE[:], AG[:, 0:WT].indirect(T.ec16[:, 0:6]), float(HALF), OP.subtract, ["AG", "AGr", "ec16"], ["AE"])
                list_arg0(T.AE, 96, ["AE"])
                ms(T.acc[:], 0.0, ["acc"] + ["acc%d" % k for k in range(16)])
                ms(T.OUT[:, W:WT], 0.0, ["Or"])
            ts(T.xc[:], U[:, W - DS:W], THUNK, OP.is_equal, ["U5"], ["xc"])
            ts(T.Pe[:, 0:96], U[:, 0:DS], HOLE, OP.not_equal, ["U0"], ["Pe"], 64.0, OP.mult)
            tt(T.Pe[:, 96:192], T.xc[:], T.am[:], OP.mult, ["xc", "am"], ["Pe"])
            if x == 0:
                ts(T.slE[:, 0:6], T.Ps[:, 0:6], float(HALF), OP.add, ["Ps"], ["slE"])
            tt(T.dsl[:, 0:6], T.slE[:, 0:6], T.slf[:, 10:16], OP.subtract, ["slE", "slf"], ["dsl"])
            after_exchange(x, total)
            fill0, fill1, fill2 = [start_guests], [], []
            if x == 2:
                for k, (a, b) in enumerate(MID):
                    dma("g", T.OUT[:, a:b], U[:, a:b], ["Um", "L2", "O%d" % k], ["O%d" % k], True)

    mm(T.Pe[:, 0:16], T.Wr[:], T.NX[:, 1:32:2], True, True, ["Wr", "NX"], ["Pe"])
    scatter_out()
    dma("y", T.yv[:, 0:HALF], T.OUT[:, 0:HALF], OK, ["yv0"])
    dma("s", T.yv[:, HALF:W], T.OUT[:, HALF:W], OK, ["yv1"])
    ts(T.s1[:], T.Pe[:, 0:16], W * X, OP.is_ge, ["Pe"], ["s1"], -8192.0 * X, OP.mult)
    tt(T.s2[:], T.s1[:], T.Pe[:, 0:16], OP.add, ["s1", "Pe"], ["s2"])
    ts(T.yo[:], T.s2[:], 1.0 / X, OP.mult, ["s2"], ["yo"], -1.0, OP.max)
    dma("y", T.ya[:], T.yo[:], ["yo"], ["ya"])
    return ops


def emit(g, T, ops):
    eng = {"v": g.vector, "s": g.scalar, "t": g.tensor, "g": g, "y": g.sync}
    writer, readers, known, clock, waits = {}, {}, {q: {} for q in eng}, [], []
    lane, pos, count, nd = [], [], {}, [0]
    for n, (q, fn, rd, wr, kind) in enumerate(ops):
        if kind == "c":
            ln = "q" + q
        elif kind == "d":
            ln = "d%d" % nd[0]
            nd[0] += 1
        else:
            ln = kind[0]
        count[ln] = count.get(ln, 0) + 1
        lane.append(ln)
        pos.append(count[ln])
        deps = set()
        for k in rd:
            if k in writer:
                deps.add(writer[k])
            if k[0] == "P":
                deps.update(r for r in readers.get(k, []) if ops[r][0] != q)
        for k in wr:
            if k in writer:
                deps.add(writer[k])
            deps.update(readers.get(k, []))
        if q == "t":
            deps = set(d for d in deps if ops[d][0] != "t")
        need = []
        if q != "x":
            kn = known[q]
            for d in sorted(deps, reverse=True):
                if kn.get(lane[d], 0) < pos[d]:
                    need.append(d)
                    for l, p in clock[d].items():
                        kn[l] = max(kn.get(l, 0), p)
            ck = dict(kn)
        else:
            ck = {}
        ck[ln] = pos[n]
        clock.append(ck)
        waits.append(need)
        for k in rd:
            readers.setdefault(k, []).append(n)
        for k in wr:
            writer[k] = n
            readers[k] = []
    signal = set(d for need in waits for d in need)
    value, total = {}, {}
    for n, (q, fn, rd, wr, kind) in enumerate(ops):
        ln = lane[n]
        if kind == "c":
            if n in signal:
                total[ln] = total.get(ln, 0) + 1
        elif kind == "d":
            total[ln] = 16
        else:
            total[ln] = kind[1]
        value[n] = total.get(ln, 0)
    for n, (q, fn, rd, wr, kind) in enumerate(ops):
        if q == "x":
            continue
        e = eng[q]
        for d in waits[n]:
            e.wait_ge(T.sem[lane[d]], value[d])
        ins = fn(e)
        if kind == "d":
            ins.then_inc(T.sem[lane[n]], 16)
        elif kind == "c" and n in signal:
            ins.then_inc(T.sem[lane[n]], 1)
    for ln in sorted(total):
        g.wait_ge(T.sem[ln], total[ln])


def rank_program(g, core, T, topo):
    if T.rank_of(core) is None:
        return
    emit(g, T, build(core, T, topo))
